import numpy as np, ml_dtypes
CORES = [35,38,43,46]
N = 4
BF = ml_dtypes.bfloat16
V, Q, RO = 512, 4, 3
W = N * V
def parts(rng):
    big = rng.permutation(np.array([1.0, 1.0, 0.8, 0.8, 0.65, 0.65, 0.5, 0.5])).reshape(1, 8, 1, 1)
    am = (256 * big * rng.random((N, 8, 1, V)) * rng.random((N, 8, 16, V))).astype(np.int64)
    o = rng.permutation(8); w = np.array([12, 12, 40, 40, 80, 80, 128, 128])[o].reshape(1, 8, 1, 1); mid = np.array([10, 10, 32, 32, 57, 57, 64, 64])[o].reshape(1, 8, 1, 1)
    ph = rng.integers(-w, w + 1, (N, 8, 16, V)) & 255
    th = np.clip((mid * (0.9 + 0.2 * rng.random((N, 8, 1, 1)))).astype(np.int64) + rng.integers(-3, 4, (N, 8, 16, 1)), 0, 128)
    return am, ph, rng.integers(0, W, (N, 8, 16, V)), th
def pack(am, ph, tr, th):
    return {"amp": np.ascontiguousarray(am.reshape(N, 128, V)).astype(np.int32), "phi": np.ascontiguousarray(ph.reshape(N, 128, V)).astype(np.int32),
            "tri": np.ascontiguousarray(tr.reshape(N, 128, V)).astype(np.int32), "th": np.ascontiguousarray(th.reshape(N, 128, 1)).astype(np.int32)}
def setup_inputs(rng):
    return pack(*parts(rng))
def setup_inputs_ties(rng):
    am, ph, tr, th = parts(rng)
    am[:, :4] = rng.permutation(np.array([0, 1, 8, 255])).reshape(1, 4, 1, 1); am[:, 4:] = 64 * rng.integers(0, 2, (N, 4, 1, V))
    p = rng.permutation(np.array([0, 1, 127, 128, 129, 255, 64, 37])); size = np.abs(((p + 128) & 255) - 128)
    ph[:] = p.reshape(1, 8, 1, 1); th[:] = size.reshape(1, 8, 1, 1); th[1::2, :, int(rng.integers(0, 16)), 0] = np.maximum(size - 1, 0)
    return pack(am, ph, tr, th)
def setup_inputs_harsh(rng):
    am, ph, tr, th = parts(rng); g = rng.permutation(8); i = int(rng.integers(0, 16))
    am[:, g[1]] = 255; am[:, g[2]] = rng.integers(0, 3, (N, 16, V)); am[:, g[2], i] = rng.integers(0, 256, (N, V))
    am[int(rng.integers(0, N))] = 0; am[:, g[0]] = 0
    th[:, g[1:]] = rng.permutation(np.array([0, 0, 0, 128, 128, 5, 30])).reshape(1, 7, 1, 1)
    return pack(am, ph, tr, th)
def setup_inputs_ends(rng):
    am, ph, tr, th = parts(rng); own = np.arange(N)[:, None, None] * V + np.arange(V)[None, None, :]
    tr[:, 0] = rng.choice(np.array([0, V - 1, V, W - V, W - 1]), (N, 16, V))
    tr[:, 1, 0::2] = own
    tr[:, 2] = ((np.arange(N) + 1) % N)[:, None, None] * V + rng.integers(0, V, (N, 16, V))
    tr[:, 3, 1::2] = tr[:, 3, 0::2]
    tr[:, 4, 2::2] = tr[:, 4, 0:1]; tr[:, 4, 3::2] = tr[:, 4, 1:2]
    tr[:, 5] = own - own % Q + rng.integers(0, Q, (N, 16, V))
    return pack(am, ph, tr, th)
def setup_inputs_bright(rng):
    am, ph, tr, th = parts(rng); own = np.arange(W).reshape(N, 1, V); g = rng.permutation(8)
    sign = rng.permutation(np.array([1, -1] * 8)).reshape(1, 1, 16, 1)
    tr[:, g[:5]] = Q * rng.integers(0, W // Q, (N, 5, 16, V)) + Q - 1
    am[:, g[:5]] = rng.integers(0, 41, (1, 5, 16, 1))
    ph[:, g[:3]] = (sign * rng.integers(105, 116, (N, 3, 16, V))) & 255
    ph[:, g[3:5]] = (sign * rng.integers(62, 67, (N, 2, 16, V))) & 255
    ph[:, g[5:]] = rng.integers(-8, 9, (N, 3, 16, V)) & 255
    th[:] = 128; th[:, g[2]] = 0; th[:, g[3], :8] = 0; th[:, g[4], 8:] = 0
    for c in g[5:]:
        lose = (np.arange(Q) == rng.integers(0, Q - 1, (W // Q, 1))).reshape(W)
        live = np.flatnonzero(~lose); lose = lose.reshape(N, 1, V)
        am[:, c] = np.where(lose, rng.integers(236, 241, (N, 16, V)), rng.integers(246, 256, (N, 16, V)))
        x = live[rng.integers(0, live.size, (N, 16, V))]
        x[:, 0::2] = np.where(lose, own, x[:, 0::2])
        tr[:, c] = x
    return pack(am, ph, tr, th)
def setup_inputs_spread(rng):
    am, ph, tr, th = parts(rng)
    am = np.minimum((np.exp2(8 * rng.random((N, 8, 1, V))) * rng.random((N, 8, 16, V))).astype(np.int64), 255)
    ph = np.floor(np.exp2(7 * rng.random((N, 8, 1, V))) * (2 * rng.random((N, 8, 16, V)) - 1)).astype(np.int64) & 255
    tr = np.minimum((W * rng.random((N, 8, 16, V)) ** 3).astype(np.int64), W - 1)
    th = np.minimum(np.exp2(7 * rng.random((N, 8, 16, 1))).astype(np.int64), 128)
    return pack(am, ph, tr, th)
def check_inputs(d):
    bad = []
    for k, lo, hi in (("amp", 0, 255), ("phi", 0, 255), ("tri", 0, W - 1), ("th", 0, 128)):
        if np.min(d[k]) < lo or np.max(d[k]) > hi: bad.append("range of " + k)
    return bad
def flat(x):
    return np.ascontiguousarray(x.astype(np.int64).reshape(N, 8, 16, V).transpose(1, 2, 0, 3)).reshape(8, 16, W)
def reference(amp, phi, tri, th):
    a0, trial, tr, lim = flat(amp), flat(phi), flat(tri), flat(np.repeat(th, V, axis=2))
    rej = np.zeros((8, W), bool)
    for rnd in range(RO):
        a = np.where(rej[:, None, :], 0, a0); lev = np.full((8, W), Q - 1)
        for t in range(Q - 1):
            s = np.zeros((8, 16, W), np.int64)
            for g in range(8):
                for m in range(8): s[g] += np.minimum(a[g][:, tr[g, 2 * m]], a[g][:, tr[g, 2 * m + 1]])
            tot = np.where(rej, -1, np.add.reduce(s, axis=1))
            tot = np.where(lev == Q - 1, tot, 2 ** 24)
            first = np.argmin(tot.reshape(8, W // Q, Q), axis=2)
            gone = (np.arange(Q) == first[:, :, None]).reshape(8, W)
            lev = np.where(gone, t, lev)
            both = np.add.reduce(s, axis=0)
            a = np.where(gone[:, None, :], 0, np.minimum(np.minimum(a, s >> 3), both >> 5))
        p = np.array(trial); phased = lev == Q - 1; fail = np.zeros((8, W), bool)
        for t in range(Q - 2, -1, -1):
            at = np.stack([np.flatnonzero(lev[g] == t) for g in range(8)])
            total = np.zeros((8, 16, W // Q), np.int64); x = np.zeros((8, 16, W // Q), np.int64)
            for g in range(8):
                h = at[g]; c = trial[g][:, h]
                for m in range(8):
                    k, l = tr[g, 2 * m][h], tr[g, 2 * m + 1][h]
                    v = (phased[g][k] & phased[g][l]).astype(np.int64)
                    dl = ((p[g][:, k] + p[g][:, l] - c + 128) & 255) - 128
                    total[g] += v * dl; x[g] += v * (np.abs(dl) - lim[g][:, h])
            y = np.add.reduce(total, axis=0)
            u = (total + (y >> 3)) >> 3
            for g in range(8):
                h = at[g]; c = trial[g][:, h]; no = np.add.reduce(x[g], axis=0) > 0
                p[g][:, h] = np.where(no, c, (c + u[g]) & 255)
                phased[g][h] = ~no; fail[g][h] = no
        rej = rej | fail
    yphi = np.ascontiguousarray(p.reshape(8, 16, N, V).transpose(2, 0, 1, 3)).reshape(N, 128, V)
    ylev = np.ascontiguousarray(lev.reshape(8, N, V).transpose(1, 0, 2))
    return {"yphi": yphi.astype(np.float32), "ylev": ylev.astype(np.float32)}

@@ -1,0 +1,528 @@
+import numpy as np
+from concourse.bass import DstId, RemoteDMATransfer
+from concourse.mybir import AluOpType as A, ActivationFunctionType as F
+
+V, NR, NP = 512, 4, 3
+W = V * NR
+NS = 6 * NP
+K = float(2 ** 42)
+BIG = 1.0e12
+
+bf, f32, i32, u16 = "bfloat16", "float32", "int32", "uint16"
+SB = {
+    "tb": (NS * W, bf), "ampi": (V, i32), "phii": (V, i32), "trii": (V, i32), "thi": (1, i32), "abi": (V, i32),
+    "ab": (V, u16), "ab2": (256, u16), "phib": (V, bf), "gb": (4096, bf), "mn": (4096, bf),
+    "di": (128, i32), "gi": (128, i32), "ti": (128, i32), "pc": (8, i32), "pf": (8, f32), "c64": (8, f32), "c2": (64, f32),
+    "i1": (128, bf), "ie": (128, bf), "i8": (128, bf), "i64": (128, bf), "ni": (128, bf), "s32": (128, bf), "s8": (128, bf),
+    "g1": (128, bf), "gk": (128, bf), "ng": (128, bf), "thm": (128, bf),
+    "pa0": (128, f32), "pa1": (128, f32), "pb0": (128, f32), "pb1": (128, f32),
+    "cb": (64, bf), "c49": (256, bf), "r256": (64, bf), "pk": (V, bf), "rst": (256, f32), "rs16": (128, f32),
+    "b4": (16, f32), "rep": (64, u16), "lc": (384, f32),
+    "pm": (V, f32), "t1": (V, f32), "t2": (V, i32), "g29": (V, bf), "kb": (V, bf), "rc": (V, bf), "al": (V, bf),
+    "z": (128, f32), "zs": (128, f32), "ri": (8, i32), "r": (16, i32), "sar": (16, f32), "sac": (16, f32), "s1": (8, f32),
+    "dd": (16, f32), "ee": (16, f32), "ff": (16, f32), "lhf": (16, f32), "lh": (16, u16), "dl": (8, f32),
+    "cf": (24, f32), "co": (24, u16), "tsel": (256, f32), "ksel": (256, bf), "psel": (256, bf), "sk": (256, bf),
+    "ll": (384, u16), "cs": (384, bf), "csf": (128, f32), "crep": (1024, bf), "q": (1024, bf), "dw": (1024, bf), "aw": (1024, bf),
+    "vv": (1024, bf), "wi": (128, i32), "pi": (128, i32), "pb": (128, bf), "rk": (128, bf),
+    "kp": (128, bf), "als": (128, bf), "ams": (128, bf), "pd": (128, f32), "pt": (128, f32), "yp": (V, f32), "lev": (V, f32),
+}
+SCRATCH = {n: ("sbuf", [128, w], d) for n, (w, d) in SB.items()}
+for _b in range(8):
+    SCRATCH["p%d" % _b] = ("psum", [128, 512], "float32")
+DMAS = ["amp", "phi", "tri", "th", "la", "lb", "oy", "ol"]
+SEMAPHORES = ["sV", "sS", "sP", "sG", "sent"] + ["d_" + d for d in DMAS] + ["arr%d" % s for s in range(NS)]
+
+
+def rank_program(g, core, T, topo):
+    rank = T.rank_of(core)
+    if rank is None:
+        return
+    Q = {"V": g.vector, "S": g.scalar, "P": g.tensor, "G": g, "Y": g.sync}
+    ENG = ["V", "S", "P", "G"]
+    width = {n: w for n, (w, d) in SB.items()}
+    width.update({"p%d" % b: 512 for b in range(8)})
+    ops = []
+    lastw = {n: np.full(w, -1) for n, w in width.items()}
+    lastr = {n: {} for n in width}
+    bank = {"p%d" % b: {} for b in range(8)}
+    clock = {q: {} for q in Q}
+
+    def v(n, a=0, b=None, s=1):
+        return (n, a, width[n] if b is None else b, s)
+
+    def ind(win, off):
+        return ("*", win, off)
+
+    def ap(x):
+        if not isinstance(x, tuple):
+            return x
+        if x[0] == "*":
+            return ap(x[1]).indirect(ap(x[2]))
+        return T[x[0]][:, x[1]:x[2]] if x[3] == 1 else T[x[0]][:, x[1]:x[2]:x[3]]
+
+    def rec(q, src, call, reads, writes, extra=()):
+        me = len(ops)
+        rd, wr = [], []
+        for x in reads:
+            if isinstance(x, tuple):
+                rd += [x[1], x[2]] if x[0] == "*" else [x]
+        for x in writes:
+            if x[0] == "*":
+                wr.append(x[1]); rd.append(x[2])
+            else:
+                wr.append(x)
+        deps = set()
+        for (n, a, b, s) in rd:
+            deps.update(np.unique(lastw[n][a:b:s]).tolist())
+        for (n, a, b, s) in wr:
+            deps.update(np.unique(lastw[n][a:b:s]).tolist())
+            for arr in lastr[n].values():
+                deps.add(int(arr[a:b:s].max()))
+        for (n, a, b, s) in rd + wr:
+            if n in bank:
+                deps.update(o for e, o in bank[n].items() if e != q)
+        deps.discard(-1)
+        best = {}
+        for d in deps:
+            sd = ops[d]["src"]
+            if sd == "R" or (sd == "P" and src == "P"):
+                continue
+            best[sd] = max(best.get(sd, -1), d)
+        waits = []
+        ck = clock[q]
+        for d in sorted(best.values(), reverse=True):
+            sd = ops[d]["src"]
+            if ck.get(sd, -1) >= d:
+                continue
+            waits.append(d)
+            ops[d]["need"] = True
+            ck[sd] = d
+            for k2, v2 in ops[d]["clock"].items():
+                ck[k2] = max(ck.get(k2, -1), v2)
+        ops.append({"q": q, "src": src, "call": call, "waits": waits, "clock": dict(ck), "need": False, "extra": list(extra)})
+        for (n, a, b, s) in rd:
+            if src not in lastr[n]:
+                lastr[n][src] = np.full(width[n], -1)
+            lastr[n][src][a:b:s] = me
+        for (n, a, b, s) in wr:
+            lastw[n][a:b:s] = me
+        for (n, a, b, s) in rd + wr:
+            if n in bank:
+                bank[n][q] = me
+        return me
+
+    pend = {"V": [], "S": []}
+
+    def take(q):
+        x = pend[q][:]
+        del pend[q][:]
+        return x
+
+    def tt(o, a, b, op):
+        rec("V", "V", lambda: g.vector.tensor_tensor(ap(o), ap(a), ap(b), op), [a, b], [o], take("V"))
+
+    def ts(o, a, s1, op0, s2=None, op1=None):
+        if op1 is None:
+            rec("V", "V", lambda: g.vector.tensor_scalar(ap(o), ap(a), ap(s1), None, op0), [a, s1], [o], take("V"))
+        else:
+            rec("V", "V", lambda: g.vector.tensor_scalar(ap(o), ap(a), ap(s1), ap(s2), op0, op1), [a, s1, s2], [o], take("V"))
+
+    def cp(o, a):
+        rec("V", "V", lambda: g.vector.tensor_copy(ap(o), ap(a)), [a], [o], take("V"))
+
+    def ms(o, c):
+        rec("V", "V", lambda: g.vector.memset(ap(o), c), [], [o])
+
+    def scan(o, d0, d1, op0, op1):
+        rec("V", "V", lambda: g.vector.tensor_tensor_scan(ap(o), ap(d0), ap(d1), 0.0, op0, op1), [d0, d1], [o])
+
+    def act(o, a, func, bias=None, scale=1.0):
+        if bias is None:
+            rec("S", "S", lambda: g.scalar.activation(ap(o), ap(a), func), [a], [o], take("S"))
+        else:
+            rec("S", "S", lambda: g.scalar.activation(ap(o), ap(a), func, bias=bias, scale=scale), [a], [o], take("S"))
+
+    def mm(o, l, r, start=False, stop=False):
+        rec("P", "P", lambda: g.tensor.matmul(ap(o), ap(v(l)), ap(r), start, stop), [v(l), r], [o])
+
+    def iota(o, pat, base, cm, fl=False):
+        if fl:
+            rec("G", "G", lambda: g.iota(ap(o), pat, base, cm, allow_small_or_imprecise_dtypes=True), [], [o])
+        else:
+            rec("G", "G", lambda: g.iota(ap(o), pat, base, cm), [], [o])
+
+    ndma = {d: 0 for d in DMAS}
+
+    def dma(q, name, o, a, reads, writes):
+        ndma[name] += 1
+        rec(q, "d_" + name, lambda: Q[q].dma_start(o, a), reads, writes)
+
+    peers = [c for c in T.cores if c != core]
+    far = [c for c in peers if topo.chip(c) != topo.chip(core)]
+    near = [c for c in peers if topo.chip(c) == topo.chip(core)]
+    off_e = topo.engines(core, far[0])
+    on_e = [e for e in topo.engines(core, near[0]) if e not in off_e]
+    route = [(far, sum(1 << e for e in off_e)), (near, sum(1 << e for e in on_e))]
+    per_send = len(off_e) + len(on_e)
+    per_arr = len(far) * len(off_e) + len(near) * len(on_e)
+    nsend = [0] * NS
+
+    def own(s, a=0, b=V, st=1):
+        return v("tb", s * W + rank * V + a, s * W + rank * V + b, st)
+
+    def tab(s):
+        return v("tb", s * W, (s + 1) * W)
+
+    def send(s, a=0, b=V):
+        x = own(s, a, b)
+        nsend[s] += 1
+
+        def call():
+            tr = []
+            for grp, m in route:
+                ids = [DstId(rid=topo.addr(c)[0], pnc=topo.addr(c)[1]) for c in grp]
+                tr.append(RemoteDMATransfer(dst_ids=ids, dma_engine_mask=m, remote_sem=T.sem["arr%d" % s],
+                                            srcs=[ap(x)], dsts=[ap(x) for c in grp]))
+            return g.remote_dma_fused(tr, local_sem=T.sem.sent)
+        rec("G", "R", call, [x], [])
+
+    def arrive(s):
+        for q in pend:
+            pend[q].append(("arr%d" % s, nsend[s] * per_arr))
+
+    dma("Y", "amp", T.ampi[:, 0:256], T.amp[:, 0:256], [], [v("ampi", 0, 256)])
+    dma("S", "amp", T.ampi[:, 256:512], T.amp[:, 256:512], [], [v("ampi", 256, 512)])
+    for k in range(4):
+        dma("S", "lb", T.abi[:, 256 + 64 * k:320 + 64 * k], T.tri[1::2, 128 * k:128 * k + 128], [], [v("abi", 256 + 64 * k, 320 + 64 * k)])
+        dma("Y", "la", T.abi[:, 64 * k:64 * k + 64], T.tri[0::2, 128 * k:128 * k + 128], [], [v("abi", 64 * k, 64 * k + 64)])
+    dma("Y", "phi", T.phii[:], T.phi[:], [], [v("phii")])
+    dma("S", "tri", T.trii[:], T.tri[:], [], [v("trii")])
+    dma("Y", "th", T.thi[:], T.th[:], [], [v("thi")])
+    iota(v("di"), [[1, 128]], 128, -1)
+    iota(v("gi"), [[16, 8], [0, 16]], 15, -1)
+    iota(v("pc", 0, 1), [[1, 1]], 0, 1)
+    iota(v("c64"), [[64, 8]], 0, 0, True)
+    iota(v("c2"), [[2, 64]], 0, 0, True)
+    ms(v("cb"), -31.0 / 64)
+    ms(v("rst"), -BIG)
+    ms(v("rs16"), 1.0)
+    for r in range(4):
+        ms(v("r256", r, 64, 4), 256.0 * r)
+    ms(v("rst", 0, 256, 4), BIG)
+    ms(v("rs16", 0, 128, 16), 0.0)
+    ts(v("i1"), v("di"), 128.0, A.is_equal)
+    ts(v("ie"), v("di"), 128.0, A.is_equal, 0.125, A.mult)
+    ts(v("ti"), v("di"), 15, A.bitwise_and)
+    cp(own(0), v("ampi"))
+    send(0)
+    ts(v("gi"), v("gi"), 4, A.arith_shift_right)
+    ts(v("s32"), v("ti"), 0.0, A.is_equal, 1.0 / 32, A.mult)
+    ts(v("gk"), v("gi"), 0.0, A.is_equal, 1024.0, A.mult)
+    cp(v("ab"), v("abi"))
+    ts(v("i64"), v("di"), 128.0, A.is_equal, 64.0, A.mult)
+    ts(v("i8"), v("di"), 128.0, A.is_equal, 8.0, A.mult)
+    ts(v("ni"), v("di"), 128.0, A.is_equal, -1.0, A.mult)
+    ts(v("s8"), v("ti"), 0.0, A.is_equal)
+    ts(v("g1"), v("gi"), 0.0, A.is_equal)
+    ts(v("ng"), v("gi"), 0.0, A.is_equal, -1.0, A.mult)
+    tt(v("s8"), v("s8"), v("i8"), A.add)
+    ts(v("pc", 1, 2), v("pc", 0, 1), 15, A.bitwise_and)
+    ts(v("pc", 2, 3), v("pc", 0, 1), 1, A.bitwise_and)
+    ts(v("pf", 0, 1), v("pc", 1, 2), 4.0, A.mult)
+    ts(v("pf", 1, 2), v("pc", 1, 2), 8.0, A.is_ge)
+    cp(v("pf", 2, 3), v("pc", 2, 3))
+    ts(v("pf", 3, 4), v("pc", 2, 3), 0.0, A.is_equal)
+    ts(v("b4", 0, 8), v("c64"), v("pf", 0, 1), A.add)
+    ts(v("b4", 8, 16), v("c64"), v("pf", 0, 1), A.add)
+
+    def late_consts():
+        ts(v("pa0"), v("di"), 128.0, A.is_equal, v("pf", 3, 4), A.mult)
+        ts(v("pa1"), v("di"), 129.0, A.is_equal, v("pf", 3, 4), A.mult)
+        ts(v("pb0"), v("di"), 127.0, A.is_equal, v("pf", 2, 3), A.mult)
+        ts(v("pb1"), v("di"), 128.0, A.is_equal, v("pf", 2, 3), A.mult)
+        ts(v("pf", 4, 5), v("thi"), -1.0, A.mult)
+        ts(v("rep"), v("c2"), v("pf", 1, 2), A.add)
+        ts(v("thm"), v("g1"), v("pf", 4, 5), A.mult)
+        ms(v("c49"), 49152.0)
+        cp(v("phib"), v("phii"))
+
+    def pick_a(src):
+        tt(v("z"), src, v("s32"), A.mult)
+
+    def pick_b():
+        scan(v("zs"), v("rs16"), v("z"), A.mult, A.add)
+
+    def lists(t):
+        cp(v("cs", 128 * t, 128 * t + 128), ind(v("phib"), v("co", 8 * t, 8 * t + 8)))
+        cp(v("ll", 128 * t, 128 * t + 128), ind(v("trii"), v("co", 8 * t, 8 * t + 8)))
+
+    def level_prep(t):
+        for h in range(2):
+            act(v("crep", 512 * h, 512 * h + 512), ind(v("cs", 128 * t, 128 * t + 128), v("rep", 32 * h, 32 * h + 32)), F.Copy)
+            for j in (2 * h, 2 * h + 1):
+                mm(v("p%d" % (4 + j), 0, 256), "i1", v("c49"), True)
+                mm(v("p%d" % (4 + j), 0, 256), "ni", v("crep", 256 * j, 256 * j + 256))
+
+    def gat(s, lst, second, c0, c1):
+        h = c0
+        if c0 == 0:
+            h = c1 // 2
+            cp(v("gb", 0, 16 * h), ind(tab(s), v(lst, second, second + h)))
+        act(v("gb", 16 * h, 16 * c1), ind(tab(s), v(lst, second + h, second + c1)), F.Copy)
+        tt(v("mn", 16 * c0, 16 * c1), ind(tab(s), v(lst, c0, c1)), v("gb", 16 * c0, 16 * c1), A.min)
+
+    PW = [("p0", 0), ("p0", 128), ("p2", 0), ("p3", 0)]
+    PS = [("p0", 256), ("p0", 384), ("p2", 128), ("p4", 0)]
+    PU = [("p1", 0), ("p1", 128), ("p2", 256), ("p5", 0)]
+    PD = [("p1", 256), ("p1", 384), ("p2", 384), ("p3", 128)]
+
+    def full_round(s, kbias):
+        def reg(P, k, e):
+            return v(P[k][0], P[k][1] + 64 * e, P[k][1] + 64 * e + 64)
+
+        def bias(P, k, e):
+            if P is PW:
+                mm(reg(P, k, e), "i1", v("r256"), True)
+                if kbias:
+                    mm(reg(P, k, e), "i1", v(kbias, 128 * k + 64 * e, 128 * k + 64 * e + 64))
+            else:
+                mm(reg(P, k, e), "i1", v("cb"), True)
+
+        def pe(k, opened=False):
+            for P, l in ((PW, "gk"), (PS, "ie"), (PU, "s32")):
+                for e in range(2):
+                    if not (opened and e == 0):
+                        bias(P, k, e)
+                    for m in range(8):
+                        mm(reg(P, k, e), l, v("mn", 1024 * k + 2 * m + e, 1024 * k + 1024, 16), False, m == 7)
+
+        def post(k, n):
+            a = 128 * k
+            x = lambda P, r=0, st=1: v(P[k][0], P[k][1] + r, P[k][1] + n, st)
+            scan(v("pm", a, a + n), v("rst", 0, n), x(PW), A.max, A.min)
+            if k < 3:
+                tt(v("t1", a, a + n), x(PS), own(s, a, a + n), A.min)
+            for r in range(4):
+                tt(x(PD, r, 4), x(PW, r, 4), v("pm", a + 3, a + n, 4), A.subtract)
+            if k == 3:
+                tt(v("t1", a, a + n), x(PS), own(s, a, a + n), A.min)
+                pick_a(v("pm", 3, V, 4))
+            tt(v("t2", a, a + n), x(PU), v("t1", a, a + n), A.min)
+            tt(own(s + 1, a, a + n), x(PD), v("t2", a, a + n), A.min)
+
+        arrive(s)
+        for k in range(3):
+            gat(s, "ab", 256, 64 * k, 64 * k + 32)
+            gat(s, "ab", 256, 64 * k + 32, 64 * k + 64)
+            pe(k)
+        post(0, 256)
+        send(s + 1, 0, 256)
+        for P in (PW, PS, PU):
+            bias(P, 3, 0)
+        gat(s, "ab", 256, 192, 256)
+        pe(3, True)
+        post(2, 128)
+        post(3, 128)
+        send(s + 1, 256, 512)
+
+    def gone_r(t):
+        pick_b()
+        ts(v("ri"), v("zs", 15, 128, 16), 0.125, A.mult)
+        ts(v("r", 8 * t, 8 * t + 8), v("ri"), 3, A.bitwise_and)
+
+    def gone_col(t):
+        tt(v("cf", 8 * t, 8 * t + 8), v("r", 8 * t, 8 * t + 8), v("b4", 0, 8), A.add)
+        cp(v("co", 8 * t, 8 * t + 8), v("cf", 8 * t, 8 * t + 8))
+
+    for ps in range(NP):
+        s0 = 6 * ps
+        last = ps == NP - 1
+        full_round(s0, "rc" if ps else None)
+        for (n, a, b, o) in (("p1", 256, 512, 0), ("p2", 384, 512, 256), ("p3", 128, 256, 384)):
+            act(v("g29", o, o + b - a), v(n, a, b), F.Relu, float(2 ** 29), -float(2 ** 21))
+        gone_r(0)
+        r0 = v("r", 0, 8)
+        ts(v("sar", 0, 8), r0, 0.0, A.is_le)
+        ts(v("sar", 8, 16), r0, 2.0, A.is_le, 2.0, A.add)
+        ts(v("s1"), r0, 1.0, A.is_le, 1.0, A.add)
+        gone_col(0)
+        if ps:
+            tt(v("kb"), v("g29"), v("rc"), A.add)
+        tt(v("sac"), v("sar"), v("b4"), A.add)
+        tt(v("dd", 0, 8), v("s1"), v("sar", 0, 8), A.subtract)
+        tt(v("dd", 8, 16), v("s1"), v("sar", 8, 16), A.subtract)
+        ms(own(s0 + 3), K)
+        if ps == 0:
+            late_consts()
+        full_round(s0 + 1, "kb" if ps else "g29")
+        gone_r(1)
+        tt(v("ee", 0, 8), v("r", 8, 16), v("sar", 0, 8), A.is_equal)
+        tt(v("ee", 8, 16), v("r", 8, 16), v("sar", 8, 16), A.is_equal)
+        tt(v("ff"), v("ee"), v("dd"), A.mult)
+        tt(v("lhf"), v("ff"), v("sac"), A.add)
+        cp(v("lh"), v("lhf"))
+        cp(v("tsel"), ind(v("trii"), v("lh")))
+        act(v("psel"), ind(v("phib"), v("lh")), F.Copy)
+        if ps:
+            act(v("ksel"), ind(v("rc"), v("lh")), F.Copy)
+        for j, (l0, l1) in enumerate((("pb0", "pb1"), ("pa0", "pa1"))):
+            o = v("p%d" % (6 + j), 0, 128)
+            mm(o, l0, v("tsel", 0, 128), True)
+            mm(o, l1, v("tsel", 128, 256), False, True)
+        gone_col(1)
+        tt(v("dl"), v("lhf", 0, 8), v("lhf", 8, 16), A.subtract)
+        cp(v("ab2", 128, 256), v("p6", 0, 128))
+        cp(v("ab2", 0, 128), v("p7", 0, 128))
+        s = s0 + 2
+        arrive(s)
+
+        def bias2(h):
+            if ps:
+                mm(v("p%d" % h, 0, 64), "i1", v("ksel", 64 * h, 64 * h + 64), True)
+                mm(v("p%d" % h, 0, 64), "ni", v("ksel", 128 + 64 * h, 192 + 64 * h))
+
+        def pe2(h):
+            for j in range(16):
+                mm(v("p%d" % h, 0, 64), "ng" if j % 2 else "g1", v("mn", 1024 * h + j, 1024 * h + 1024, 16), j == 0 and ps == 0, j == 15)
+
+        def post2(h):
+            for e, op in ((0, A.is_le), (1, A.is_gt)):
+                ts(v("sk", 128 * e + 64 * h, 128 * e + 64 * h + 64), v("p%d" % h, 0, 64), 0.0, op, K, A.mult)
+            for e in range(2):
+                a = 128 * e + 64 * h
+                tt(ind(own(s + 1), v("lh", 8 * e + 4 * h, 8 * e + 4 * h + 4)), v("psel", a, a + 64), v("sk", a, a + 64), A.add)
+
+        bias2(0)
+        bias2(1)
+        gat(s, "ab2", 128, 0, 32)
+        gat(s, "ab2", 128, 32, 64)
+        pe2(0)
+        gat(s, "ab2", 128, 64, 96)
+        gat(s, "ab2", 128, 96, 128)
+        pe2(1)
+        post2(0)
+        post2(1)
+        send(s + 1)
+        pick_a(v("sk", 0, 128))
+        pick_b()
+        tt(v("ff", 0, 8), v("zs", 15, 128, 16), v("dl"), A.mult)
+        ts(v("ff", 0, 8), v("ff", 0, 8), 32.0 / K, A.mult)
+        tt(v("cf", 16, 24), v("ff", 0, 8), v("lhf", 8, 16), A.add)
+        cp(v("co", 16, 24), v("cf", 16, 24))
+        lists(2)
+        level_prep(2)
+        cp(own(s + 2), own(s + 1))
+        lists(1)
+        if ps == 0:
+            ms(v("al"), 1.0)
+        if last:
+            cp(v("yp"), v("phii"))
+        for t in (2, 1, 0):
+            s = s0 + 5 - t
+            col = v("co", 8 * t, 8 * t + 8)
+            cs = v("cs", 128 * t, 128 * t + 128)
+            phase = last or t > 0
+            arrive(s)
+            E = lambda j: v("p%d" % (4 + j), 0, 256)
+            H = lambda n, j, k=1: v(n, 256 * j, 256 * (j + k))
+            if phase:
+                mm(v("p0", 0, 64), "i64", v("cs", 128 * t, 128 * t + 64), True)
+            for j in range(4):
+                o, a = v("gb", 512 * j, 512 * j + 512), ind(tab(s), v("ll", 128 * t + 32 * j, 128 * t + 32 * j + 32))
+                if j % 2:
+                    act(o, a, F.Copy)
+                else:
+                    cp(o, a)
+                for u in range(2):
+                    mm(E(j), "i1", v("gb", 512 * j + u, 512 * j + 512, 2), False, u == 1)
+
+            def sums(b, h, l, src, start, stop):
+                for m in range(8):
+                    mm(v(b, 64 * h, 64 * h + 64), l, v(src, 512 * h + m, 512 * h + 512, 8), start and m == 0, stop and m == 7)
+
+            ts(H("q", 0), E(0), 0.5, A.add)
+            for j in (1, 2, 3):
+                act(H("q", j), E(j), F.Identity, 0.5)
+            for h in range(2):
+                for j in (2 * h, 2 * h + 1):
+                    tt(H("dw", j), E(j), H("q", j), A.subtract)
+                    if h:
+                        act(H("aw", j), H("dw", j), F.Abs)
+                if h == 0:
+                    act(H("aw", 0, 2), H("dw", 0, 2), F.Abs)
+                ts(H("vv", 2 * h, 2), H("q", 2 * h, 2), float(2 ** 20), A.is_lt)
+                if phase:
+                    if h:
+                        mm(v("p0", 64, 128), "i64", v("cs", 128 * t + 64, 128 * t + 128), True)
+                    sums("p0", h, "s8", "dw", False, True)
+                sums("p1", h, "thm", "vv", True, False)
+                sums("p1", h, "g1", "aw", False, True)
+            X = v("p1", 0, 128)
+            if phase:
+                cp(v("wi"), v("p0", 0, 128))
+                ts(v("pi"), v("wi"), 6, A.arith_shift_right, 255, A.bitwise_and)
+            if t > 0:
+                cp(v("pb"), v("pi"))
+                ts(v("rk"), X, 0.0, A.is_gt, K, A.mult)
+                tt(ind(own(s + 1), col), v("pb"), v("rk"), A.add)
+                send(s + 1)
+                level_prep(t - 1)
+                if t == 2:
+                    cp(own(s + 2), own(s + 1))
+                    lists(0)
+            if last:
+                if t == 2:
+                    cp(v("csf"), cs)
+                tt(v("pd"), v("pi"), cs, A.subtract)
+                ts(v("p2", 0, 128), X, 0.0, A.is_le)
+                tt(v("pt"), v("p2", 0, 128), v("pd"), A.mult)
+                tt(ind(v("yp"), col), v("pt"), v("csf"), A.add)
+                if t > 0:
+                    cp(v("csf"), v("cs", 128 * t - 128, 128 * t))
+                if t == 2:
+                    ms(v("lev"), 3.0)
+                    for u in range(3):
+                        ms(v("lc", 128 * u, 128 * u + 128), float(u))
+                if t == 1:
+                    for u in range(3):
+                        cp(ind(v("lev"), v("co", 8 * u, 8 * u + 8)), v("lc", 128 * u, 128 * u + 128))
+                    for c in range(8):
+                        dma("Y", "ol", T.ylev[c:c + 1, :], T.lev[16 * c:16 * c + 1, :], [v("lev")], [])
+                if t == 0:
+                    dma("Y", "oy", T.yphi[:], T.yp[:], [v("yp")], [])
+            else:
+                ts(v("kp"), X, 0.0, A.is_le)
+                if t == 0:
+                    tt(ind(own(s + 1), col), v("ams"), v("kp"), A.mult)
+                    send(s + 1)
+                cp(v("als"), ind(v("al"), col))
+                tt(ind(v("al"), col), v("als"), v("kp"), A.mult)
+                if t == 1:
+                    tt(own(s + 2), own(0), v("al"), A.mult)
+                    cp(v("ams"), ind(own(s + 2), v("co", 0, 8)))
+                if t == 2 and ps == 0:
+                    for r in range(4):
+                        ms(v("pk", r, V, 4), float((4 - r) * 2 ** 26))
+                if t == 0:
+                    ts(v("kb"), v("al"), -1.0, A.add)
+                    tt(v("rc"), v("kb"), v("pk"), A.mult)
+
+    count = {e: 0 for e in ENG}
+    val = {}
+    for i, o in enumerate(ops):
+        q, src = Q[o["q"]], o["src"]
+        for d in o["waits"]:
+            q.wait_ge(*val[d])
+        for name, n in o["extra"]:
+            q.wait_ge(T.sem[name], n)
+        ins = o["call"]()
+        if src.startswith("d_"):
+            ins.then_inc(T.sem[src], 16)
+            val[i] = (T.sem[src], 16 * ndma[src[2:]])
+        elif src != "R" and o["need"]:
+            count[src] += 1
+            ins.then_inc(T.sem["s" + src], 1)
+            val[i] = (T.sem["s" + src], count[src])
+    g.wait_ge(T.sem.sent, sum(nsend) * per_send)
+    g.sync.wait_ge(T.sem.d_ol, 16 * ndma["ol"])
+    g.sync.wait_ge(T.sem.d_oy, 16 * ndma["oy"])

@@ -6,30 +6,34 @@ V, NR, NP = 512, 4, 3
 W = V * NR
 NS = 6 * NP
 K = float(2 ** 42)
-BIG = 1.0e12
+M1 = 1.5 * 2 ** 23
+M8 = 1.5 * 2 ** 31
+PAIRS = [(0, 1), (0, 2), (0, 3), (1, 2), (1, 3), (2, 3)]
 
-bf, f32, i32, u16 = "bfloat16", "float32", "int32", "uint16"
+bf, f32, i32, u16, f16 = "bfloat16", "float32", "int32", "uint16", "float16"
 SB = {
-    "tb": (NS * W, bf), "ampi": (V, i32), "phii": (V, i32), "trii": (V, i32), "thi": (1, i32), "abi": (V, i32),
+    "tb": (NS * W, bf), "ampi": (V, i32), "phii": (V, i32), "trii": (V, i32), "thi": (1, i32),
+    "tB": (V, i32), "tC": (V, f32), "tD": (V, f32), "li": (64, i32), "lu": (64, u16),
     "ab": (V, u16), "ab2": (256, u16), "phib": (V, bf), "gb": (4096, bf), "mn": (4096, bf),
-    "di": (128, i32), "gi": (128, i32), "ti": (128, i32), "pc": (8, i32), "pf": (8, f32), "c64": (8, f32), "c2": (64, f32),
-    "i1": (128, bf), "ie": (128, bf), "i8": (128, bf), "i64": (128, bf), "ni": (128, bf), "s32": (128, bf), "s8": (128, bf),
-    "g1": (128, bf), "gk": (128, bf), "ng": (128, bf), "thm": (128, bf),
-    "pa0": (128, f32), "pa1": (128, f32), "pb0": (128, f32), "pb1": (128, f32),
-    "cb": (64, bf), "c49": (256, bf), "r256": (64, bf), "pk": (V, bf), "rst": (256, f32), "rs16": (128, f32),
-    "b4": (16, f32), "rep": (64, u16), "lc": (384, f32),
-    "pm": (V, f32), "t1": (V, f32), "t2": (V, i32), "g29": (V, bf), "kb": (V, bf), "rc": (V, bf), "al": (V, bf),
-    "z": (128, f32), "zs": (128, f32), "ri": (8, i32), "r": (16, i32), "sar": (16, f32), "sac": (16, f32), "s1": (8, f32),
-    "dd": (16, f32), "ee": (16, f32), "ff": (16, f32), "lhf": (16, f32), "lh": (16, u16), "dl": (8, f32),
-    "cf": (24, f32), "co": (24, u16), "tsel": (256, f32), "ksel": (256, bf), "psel": (256, bf), "sk": (256, bf),
-    "ll": (384, u16), "cs": (384, bf), "csf": (128, f32), "crep": (1024, bf), "q": (1024, bf), "dw": (1024, bf), "aw": (1024, bf),
-    "vv": (1024, bf), "wi": (128, i32), "pi": (128, i32), "pb": (128, bf), "rk": (128, bf),
+    "di": (144, i32), "gi": (128, i32), "ti": (128, i32), "gg": (24, i32), "pc": (8, i32), "pf": (16, f32), "c64": (8, f32),
+    "i1": (128, bf), "ie": (128, bf), "i2": (128, bf), "i3": (128, bf), "i4": (128, bf), "ni": (128, bf), "s8": (128, bf),
+    "g1": (128, bf), "g2": (128, bf), "ng": (128, bf), "thm": (V, bf), "zz": (144, bf), "sm": (256, bf), "brow": (128, bf),
+    "lt": (V, bf), "lb": (V, bf), "eu": (V, bf), "ed": (V, bf),
+    "pa0": (128, f16), "pa1": (128, f16), "pb0": (128, f16), "pb1": (128, f16),
+    "cb": (256, bf), "cb2": (128, bf), "c25": (128, bf), "cd": (64, bf), "cm": (64, bf), "cm2": (128, bf), "cap": (1, f32),
+    "c49": (256, bf), "r256": (256, bf), "pk": (V, bf), "rs16": (256, bf), "thb": (2, bf), "thw": (4, i32),
+    "b4": (16, f32), "lc": (384, f32),
+    "cl": (128, bf), "t1": (V, i32), "t2": (V, bf), "x0": (V, bf), "x1": (V, bf), "yy": (V, bf), "kb": (V, bf), "rc": (V, bf), "al": (V, bf),
+    "z": (256, f32), "zs": (256, f32), "zb": (256, bf), "zsb": (256, bf), "ff": (16, f32), "lhf": (16, f32), "lh": (16, u16),
+    "cf": (8, f32), "co": (24, u16), "tsel": (256, f16), "ksel": (256, bf), "psel": (256, bf), "sk": (256, bf),
+    "ll": (384, u16), "cs": (384, bf), "csf": (128, f32), "q": (1024, bf), "dw": (1024, bf), "aw": (1024, bf),
+    "vc": (64, bf), "wi": (128, i32), "pi": (128, i32), "pq": (128, bf), "pb": (128, bf), "rk": (128, bf),
     "kp": (128, bf), "als": (128, bf), "ams": (128, bf), "pd": (128, f32), "pt": (128, f32), "yp": (V, f32), "lev": (V, f32),
 }
 SCRATCH = {n: ("sbuf", [128, w], d) for n, (w, d) in SB.items()}
 for _b in range(8):
     SCRATCH["p%d" % _b] = ("psum", [128, 512], "float32")
-DMAS = ["amp", "phi", "tri", "th", "la", "lb", "oy", "ol"]
+DMAS = ["amp", "phi", "tri", "th", "la", "oy", "ol"]
 SEMAPHORES = ["sV", "sS", "sP", "sG", "sent"] + ["d_" + d for d in DMAS] + ["arr%d" % s for s in range(NS)]
 
 
@@ -133,6 +137,9 @@ def rank_program(g, core, T, topo):
     def ms(o, c):
         rec("V", "V", lambda: g.vector.memset(ap(o), c), [], [o])
 
+    def ms_hi(n, c):
+        rec("V", "V", lambda: g.vector.memset(T[n][64:128, :], c), [], [v(n)])
+
     def scan(o, d0, d1, op0, op1):
         rec("V", "V", lambda: g.vector.tensor_tensor_scan(ap(o), ap(d0), ap(d1), 0.0, op0, op1), [d0, d1], [o])
 
@@ -140,10 +147,11 @@ def rank_program(g, core, T, topo):
         if bias is None:
             rec("S", "S", lambda: g.scalar.activation(ap(o), ap(a), func), [a], [o], take("S"))
         else:
-            rec("S", "S", lambda: g.scalar.activation(ap(o), ap(a), func, bias=bias, scale=scale), [a], [o], take("S"))
+            rec("S", "S", lambda: g.scalar.activation(ap(o), ap(a), func, bias=bias, scale=ap(scale)), [a, scale], [o], take("S"))
 
     def mm(o, l, r, start=False, stop=False):
-        rec("P", "P", lambda: g.tensor.matmul(ap(o), ap(v(l)), ap(r), start, stop), [v(l), r], [o])
+        l = v(l) if isinstance(l, str) else l
+        rec("P", "P", lambda: g.tensor.matmul(ap(o), ap(l), ap(r), start, stop), [l, r], [o])
 
     def iota(o, pat, base, cm, fl=False):
         if fl:
@@ -153,9 +161,9 @@ def rank_program(g, core, T, topo):
 
     ndma = {d: 0 for d in DMAS}
 
-    def dma(q, name, o, a, reads, writes):
+    def dma(q, name, o, a, reads, writes, extra=()):
         ndma[name] += 1
-        rec(q, "d_" + name, lambda: Q[q].dma_start(o, a), reads, writes)
+        rec(q, "d_" + name, lambda: Q[q].dma_start(o, a), reads, writes, extra)
 
     peers = [c for c in T.cores if c != core]
     far = [c for c in peers if topo.chip(c) != topo.chip(core)]
@@ -192,76 +200,133 @@ def rank_program(g, core, T, topo):
 
     dma("Y", "amp", T.ampi[:, 0:256], T.amp[:, 0:256], [], [v("ampi", 0, 256)])
     dma("S", "amp", T.ampi[:, 256:512], T.amp[:, 256:512], [], [v("ampi", 256, 512)])
-    for k in range(4):
-        dma("S", "lb", T.abi[:, 256 + 64 * k:320 + 64 * k], T.tri[1::2, 128 * k:128 * k + 128], [], [v("abi", 256 + 64 * k, 320 + 64 * k)])
-        dma("Y", "la", T.abi[:, 64 * k:64 * k + 64], T.tri[0::2, 128 * k:128 * k + 128], [], [v("abi", 64 * k, 64 * k + 64)])
-    dma("Y", "phi", T.phii[:], T.phi[:], [], [v("phii")])
-    dma("S", "tri", T.trii[:], T.tri[:], [], [v("trii")])
-    dma("Y", "th", T.thi[:], T.th[:], [], [v("thi")])
-    iota(v("di"), [[1, 128]], 128, -1)
-    iota(v("gi"), [[16, 8], [0, 16]], 15, -1)
+    for c in range(8):
+        a, e = c // 2, c % 2
+        dma("YS"[e], "la", T.tB[32 * a:32 * a + 32, 256 * e:256 * e + 256], T.tri[16 * c:16 * c + 16, :], [],
+            [v("tB", 256 * e + a, 256 * e + 256, 4)])
+    iota(v("di"), [[1, 144]], 128, -1)
     iota(v("pc", 0, 1), [[1, 1]], 0, 1)
+    iota(v("gg"), [[0, 3], [16, 8]], 15, -1)
+    iota(v("li", 0, 32), [[16, 16], [256, 2]], 0, 0)
+    iota(v("li", 32, 64), [[2, 2], [1, 2], [4, 8]], 0, 0)
+    iota(v("gi"), [[16, 8], [0, 16]], 15, -1)
     iota(v("c64"), [[64, 8]], 0, 0, True)
-    iota(v("c2"), [[2, 64]], 0, 0, True)
+    d128 = v("di", 0, 128)
     ms(v("cb"), -31.0 / 64)
-    ms(v("rst"), -BIG)
-    ms(v("rs16"), 1.0)
+    ms(v("lt"), 0.0)
+    ms(v("cd"), -31.0 / 64)
+    ms(v("cm"), M1)
+    ms(v("cap"), 255.0)
     for r in range(4):
-        ms(v("r256", r, 64, 4), 256.0 * r)
-    ms(v("rst", 0, 256, 4), BIG)
-    ms(v("rs16", 0, 128, 16), 0.0)
-    ts(v("i1"), v("di"), 128.0, A.is_equal)
-    ts(v("ie"), v("di"), 128.0, A.is_equal, 0.125, A.mult)
-    ts(v("ti"), v("di"), 15, A.bitwise_and)
+        ms(v("r256", r, 256, 4), 256.0 * r)
+    ms_hi("cd", -1.0)
+    ms_hi("cm", 0.0)
+    ms_hi("cap", 1.0)
+    ts(v("ti"), d128, 15, A.bitwise_and)
+    ts(v("pc", 1, 2), v("pc", 0, 1), 15, A.bitwise_and)
+    ts(v("gg"), v("gg"), 4, A.arith_shift_right)
+    ts(v("i1"), d128, 128.0, A.is_equal)
+    cp(v("pf", 0, 1), v("pc", 1, 2))
+    ts(v("pf", 1, 2), v("pc", 1, 2), 32.0, A.mult)
+    ts(v("ie"), d128, 128.0, A.is_equal, 0.125, A.mult)
+    ts(v("ni"), d128, 128.0, A.is_equal, -1.0, A.mult)
     cp(own(0), v("ampi"))
     send(0)
-    ts(v("gi"), v("gi"), 4, A.arith_shift_right)
-    ts(v("s32"), v("ti"), 0.0, A.is_equal, 1.0 / 32, A.mult)
-    ts(v("gk"), v("gi"), 0.0, A.is_equal, 1024.0, A.mult)
-    cp(v("ab"), v("abi"))
-    ts(v("i64"), v("di"), 128.0, A.is_equal, 64.0, A.mult)
-    ts(v("i8"), v("di"), 128.0, A.is_equal, 8.0, A.mult)
-    ts(v("ni"), v("di"), 128.0, A.is_equal, -1.0, A.mult)
-    ts(v("s8"), v("ti"), 0.0, A.is_equal)
-    ts(v("g1"), v("gi"), 0.0, A.is_equal)
-    ts(v("ng"), v("gi"), 0.0, A.is_equal, -1.0, A.mult)
-    tt(v("s8"), v("s8"), v("i8"), A.add)
-    ts(v("pc", 1, 2), v("pc", 0, 1), 15, A.bitwise_and)
-    ts(v("pc", 2, 3), v("pc", 0, 1), 1, A.bitwise_and)
-    ts(v("pf", 0, 1), v("pc", 1, 2), 4.0, A.mult)
-    ts(v("pf", 1, 2), v("pc", 1, 2), 8.0, A.is_ge)
-    cp(v("pf", 2, 3), v("pc", 2, 3))
-    ts(v("pf", 3, 4), v("pc", 2, 3), 0.0, A.is_equal)
-    ts(v("b4", 0, 8), v("c64"), v("pf", 0, 1), A.add)
-    ts(v("b4", 8, 16), v("c64"), v("pf", 0, 1), A.add)
+    iota(v("brow"), [[1, 128]], 0, 0, True)
+    ts(v("lu", 0, 32), v("li", 0, 32), v("pf", 0, 1), A.add)
+    ts(v("lu", 32, 64), v("li", 32, 64), v("pf", 1, 2), A.add)
+    for r in range(4):
+        ts(v("lt", 144 * r, 144 * r + 16), v("ti", 0, 16), 0.0, A.is_equal, 1.0 / 32, A.mult)
+        qs = [(q, 2.0 if a == r else -2.0) for q, (a, b) in enumerate(PAIRS) if r in (a, b)]
+        runs = []
+        for q, sg in qs:
+            if runs and runs[-1][1] == q and runs[-1][2] == sg:
+                runs[-1][1] = q + 1
+            else:
+                runs.append([q, q + 1, sg])
+        for q0, q1, sg in runs:
+            ts(v("lt", 128 * r + 64 + 8 * q0, 128 * r + 64 + 8 * q1), v("gg", 0, 8 * (q1 - q0)), 0.0, A.is_equal, sg, A.mult)
+    ts(v("pf", 2, 3), v("pc", 0, 1), 64.0, A.is_lt, 32.0, A.mult)
+    ts(v("pf", 3, 4), v("pc", 0, 1), 64.0, A.is_ge, 128.0, A.mult)
+    for r in range(4):
+        mm(v("p7", 128 * r, 128 * r + 128), v("lt", 128 * r, 128 * r + 128), v("i1"), True, True)
+    act(v("eu"), v("p7"), F.Identity, 0.0, v("pf", 2, 3))
+    act(v("ed"), v("p7"), F.Identity, 0.0, v("pf", 3, 4))
+    cp(v("tC"), ind(v("tB"), v("lu", 0, 32)))
+    rec("V", "V", lambda: g.vector.transpose(T.tD[:], T.tC[:]), [v("tC")], [v("tD")])
+    cp(v("ab"), ind(v("tD"), v("lu", 32, 64)))
+    ts(v("sm", 0, 128), v("ti"), 0.0, A.is_equal)
+    ts(v("sm", 128, 256), v("ti"), 0.0, A.is_equal)
+    ms(v("rs16"), 1.0)
+    ts(v("i2"), d128, 128.0, A.is_equal, 2.0, A.mult)
+    ms(v("rs16", 0, 256, 16), 0.0)
+    ts(v("i3"), d128, 128.0, A.is_equal, 3.0, A.mult)
+    ts(v("i4"), d128, 128.0, A.is_equal, 4.0, A.mult)
+    ms(v("lb"), 0.0)
+    for r in range(4):
+        act(v("lb", 128 * r + 64, 128 * r + 112), v("lt", 128 * r + 64, 128 * r + 112), F.Identity, 0.0, 65536.0)
+
+    def late_loads():
+        x = [("arr0", nsend[0] * per_arr)]
+        dma("Y", "tri", T.trii[:], T.tri[:], [], [v("trii")], x)
+        dma("Y", "phi", T.phii[:], T.phi[:], [], [v("phii")])
+        dma("Y", "th", T.thi[:], T.th[:], [], [v("thi")])
 
     def late_consts():
-        ts(v("pa0"), v("di"), 128.0, A.is_equal, v("pf", 3, 4), A.mult)
-        ts(v("pa1"), v("di"), 129.0, A.is_equal, v("pf", 3, 4), A.mult)
-        ts(v("pb0"), v("di"), 127.0, A.is_equal, v("pf", 2, 3), A.mult)
-        ts(v("pb1"), v("di"), 128.0, A.is_equal, v("pf", 2, 3), A.mult)
-        ts(v("pf", 4, 5), v("thi"), -1.0, A.mult)
-        ts(v("rep"), v("c2"), v("pf", 1, 2), A.add)
-        ts(v("thm"), v("g1"), v("pf", 4, 5), A.mult)
-        ms(v("c49"), 49152.0)
+        ts(v("gi"), v("gi"), 4, A.arith_shift_right)
+        ts(v("pc", 2, 3), v("pc", 0, 1), 1, A.bitwise_and)
+        ts(v("pf", 4, 5), v("pc", 1, 2), 4.0, A.mult)
+        cp(v("pf", 7, 8), v("thi"))
+        ts(v("g1"), v("gi"), 0.0, A.is_equal)
+        cp(v("pf", 5, 6), v("pc", 2, 3))
+        ts(v("pf", 6, 7), v("pc", 2, 3), 0.0, A.is_equal)
+        ts(v("thb"), v("c64", 0, 2), 0.0, A.mult, v("pf", 7, 8), A.add)
+        ts(v("b4", 0, 8), v("c64"), v("pf", 4, 5), A.add)
+        ts(v("b4", 8, 16), v("c64"), v("pf", 4, 5), A.add, 3.0, A.add)
+        mm(v("p5", 256, 258), "g1", v("thb"), True, True)
+        ts(v("pa0"), d128, 128.0, A.is_equal, v("pf", 6, 7), A.mult)
+        ts(v("pa1"), d128, 129.0, A.is_equal, v("pf", 6, 7), A.mult)
+        ts(v("pb0"), d128, 127.0, A.is_equal, v("pf", 5, 6), A.mult)
+        ts(v("pb1"), d128, 128.0, A.is_equal, v("pf", 5, 6), A.mult)
+        cp(v("thw", 0, 2), v("p5", 256, 258))
+        ms(v("c25"), -2.5)
+        act(v("ng"), v("g1"), F.Identity, 0.0, -1.0)
         cp(v("phib"), v("phii"))
 
-    def pick_a(src):
-        tt(v("z"), src, v("s32"), A.mult)
-
-    def pick_b():
-        scan(v("zs"), v("rs16"), v("z"), A.mult, A.add)
+    def later_consts():
+        ts(v("thw", 2, 3), v("thw", 0, 1), 4, A.arith_shift_right)
+        ts(v("thw", 3, 4), v("thw", 0, 1), 15, A.bitwise_and)
+        ts(v("pf", 8, 9), v("pc", 1, 2), 8.0, A.is_lt)
+        ts(v("pf", 9, 10), v("pc", 1, 2), 8.0, A.is_ge)
+        ts(v("pf", 14, 15), v("pc", 1, 2), 0.0, A.is_equal)
+        for h in range(2):
+            ts(v("pf", 10 + 2 * h, 11 + 2 * h), v("thw", 2, 3), -16.0, A.mult, v("pf", 8 + h, 9 + h), A.mult)
+            ts(v("pf", 11 + 2 * h, 12 + 2 * h), v("thw", 3, 4), -1.0, A.mult, v("pf", 8 + h, 9 + h), A.mult)
+        ts(v("zz"), v("di"), 144.0, A.is_equal, v("pf", 14, 15), A.mult)
+        for u in range(4):
+            act(v("thm", 128 * u, 128 * u + 128), v("g1"), F.Identity, 0.0, v("pf", 10 + u, 11 + u))
+        act(v("g2"), v("g1"), F.Identity, 0.0, 2.0)
+        ts(v("s8"), v("ti"), 0.0, A.is_equal, 1.0 / 64, A.mult)
+        ms(v("c49"), 49152.0)
+        ms(v("cb2"), -63.0 / 128)
+        ms(v("cm2"), M1)
+        tt(v("s8"), v("s8"), v("ie"), A.add)
 
     def lists(t):
         cp(v("cs", 128 * t, 128 * t + 128), ind(v("phib"), v("co", 8 * t, 8 * t + 8)))
         cp(v("ll", 128 * t, 128 * t + 128), ind(v("trii"), v("co", 8 * t, 8 * t + 8)))
 
-    def level_prep(t):
-        for h in range(2):
-            act(v("crep", 512 * h, 512 * h + 512), ind(v("cs", 128 * t, 128 * t + 128), v("rep", 32 * h, 32 * h + 32)), F.Copy)
-            for j in (2 * h, 2 * h + 1):
-                mm(v("p%d" % (4 + j), 0, 256), "i1", v("c49"), True)
-                mm(v("p%d" % (4 + j), 0, 256), "ni", v("crep", 256 * j, 256 * j + 256))
+    def level_prep(t, phase):
+        for j in range(4):
+            mm(v("p%d" % (4 + j), 0, 256), "i1", v("c49"), True)
+            for m in range(4):
+                mm(v("p%d" % (4 + j), 64 * m, 64 * m + 64), "ni", v("cs", 128 * t + 64 * (j // 2), 128 * t + 64 * (j // 2) + 64))
+
+    def level_open(t, phase):
+        mm(v("p1", 0, 128), "i1", v("cb2"), True)
+        if phase:
+            mm(v("p0", 0, 128), "i1", v("cb2"), True)
+            mm(v("p0", 0, 128), "i1", v("cs", 128 * t, 128 * t + 128))
 
     def gat(s, lst, second, c0, c1):
         h = c0
@@ -271,148 +336,191 @@ def rank_program(g, core, T, topo):
         act(v("gb", 16 * h, 16 * c1), ind(tab(s), v(lst, second + h, second + c1)), F.Copy)
         tt(v("mn", 16 * c0, 16 * c1), ind(tab(s), v(lst, c0, c1)), v("gb", 16 * c0, 16 * c1), A.min)
 
-    PW = [("p0", 0), ("p0", 128), ("p2", 0), ("p3", 0)]
-    PS = [("p0", 256), ("p0", 384), ("p2", 128), ("p4", 0)]
-    PU = [("p1", 0), ("p1", 128), ("p2", 256), ("p5", 0)]
-    PD = [("p1", 256), ("p1", 384), ("p2", 384), ("p3", 128)]
+    PS = lambda h: v("p%d" % h, 0, 256)
+    DU = lambda h: v("p%d" % (2 + h), 0, 64)
+    PU = lambda h, r=0, st=1: v("p%d" % (4 + h), r, 256, st)
+    PD = lambda h, r=0, st=1: v("p%d" % (6 + h), r, 256, st)
+    wt = lambda n, r: v(n, 128 * r, 128 * r + 128)
 
-    def full_round(s, kbias):
-        def reg(P, k, e):
-            return v(P[k][0], P[k][1] + 64 * e, P[k][1] + 64 * e + 64)
+    def full_round(s, biases):
+        for h in range(2):
+            mm(PS(h), "i1", v("cb"), True)
+            mm(DU(h), "i1", v("cd"), True)
+            for kb in biases:
+                for r in range(4):
+                    mm(DU(h), wt("lb", r), v(kb, 256 * h + r, 256 * h + 256, 4))
+        for h in range(2):
+            mm(PD(h), "i1", v("r256"), True)
 
-        def bias(P, k, e):
-            if P is PW:
-                mm(reg(P, k, e), "i1", v("r256"), True)
-                if kbias:
-                    mm(reg(P, k, e), "i1", v(kbias, 128 * k + 64 * e, 128 * k + 64 * e + 64))
-            else:
-                mm(reg(P, k, e), "i1", v("cb"), True)
+        def piece(h, m0, m1):
+            gat(s, "ab", 256, 128 * h + 16 * m0, 128 * h + 16 * m1)
+            for m in range(m0, m1):
+                a = 2048 * h + 256 * m
+                for r in range(4):
+                    mm(DU(h), wt("lt", r), v("mn", a + r, a + 256, 4))
+                if m == 7:
+                    mm(DU(h), "i1", v("cm"))
+                    mm(DU(h), "ni", v("cm"), False, True)
+                mm(PS(h), "ie", v("mn", a, a + 256), False, m == 7)
 
-        def pe(k, opened=False):
-            for P, l in ((PW, "gk"), (PS, "ie"), (PU, "s32")):
-                for e in range(2):
-                    if not (opened and e == 0):
-                        bias(P, k, e)
-                    for m in range(8):
-                        mm(reg(P, k, e), l, v("mn", 1024 * k + 2 * m + e, 1024 * k + 1024, 16), False, m == 7)
-
-        def post(k, n):
-            a = 128 * k
-            x = lambda P, r=0, st=1: v(P[k][0], P[k][1] + r, P[k][1] + n, st)
-            scan(v("pm", a, a + n), v("rst", 0, n), x(PW), A.max, A.min)
-            if k < 3:
-                tt(v("t1", a, a + n), x(PS), own(s, a, a + n), A.min)
+        def clamp(h):
+            c = v("cl", 64 * h, 64 * h + 64)
+            ts(c, DU(h), 0.0, A.max, v("cap"), A.min)
             for r in range(4):
-                tt(x(PD, r, 4), x(PW, r, 4), v("pm", a + 3, a + n, 4), A.subtract)
-            if k == 3:
-                tt(v("t1", a, a + n), x(PS), own(s, a, a + n), A.min)
-                pick_a(v("pm", 3, V, 4))
-            tt(v("t2", a, a + n), x(PU), v("t1", a, a + n), A.min)
-            tt(own(s + 1, a, a + n), x(PD), v("t2", a, a + n), A.min)
+                mm(PU(h, r, 4), wt("eu", r), c, True, True)
+            for r in range(4):
+                mm(PD(h, r, 4), wt("ed", r), c, False, r == 3)
+
+        hf = lambda n, h: v(n, 256 * h, 256 * h + 256)
+        m1 = lambda h: tt(hf("t1", h), PS(h), own(s, 256 * h, 256 * h + 256), A.min)
+        m2 = lambda h: tt(hf("t2", h), PU(h), hf("t1", h), A.min)
+        m3 = lambda h: tt(own(s + 1, 256 * h, 256 * h + 256), PD(h), hf("t2", h), A.min)
 
         arrive(s)
-        for k in range(3):
-            gat(s, "ab", 256, 64 * k, 64 * k + 32)
-            gat(s, "ab", 256, 64 * k + 32, 64 * k + 64)
-            pe(k)
-        post(0, 256)
+        for m in range(0, 8, 2):
+            piece(0, m, m + 2)
+        piece(1, 0, 2)
+        clamp(0)
+        m1(0)
+        piece(1, 2, 4)
+        m2(0)
+        piece(1, 4, 6)
+        m3(0)
         send(s + 1, 0, 256)
-        for P in (PW, PS, PU):
-            bias(P, 3, 0)
-        gat(s, "ab", 256, 192, 256)
-        pe(3, True)
-        post(2, 128)
-        post(3, 128)
+        piece(1, 6, 7)
+        piece(1, 7, 8)
+        clamp(1)
+        m1(1)
+        m2(1)
+        m3(1)
         send(s + 1, 256, 512)
 
-    def gone_r(t):
-        pick_b()
-        ts(v("ri"), v("zs", 15, 128, 16), 0.125, A.mult)
-        ts(v("r", 8 * t, 8 * t + 8), v("ri"), 3, A.bitwise_and)
+    def gone(x, t):
+        for h in range(2):
+            act(v(x, 256 * h, 256 * h + 256), PD(h), F.Relu, 1.0, -1.0 / 256)
+        o = v("p3", 256, 384)
+        mm(o, "i4", v("brow"), True)
+        for r in (1, 2, 3):
+            mm(o, "i%d" % r, v(x, r, V, 4), False, r == 3)
 
-    def gone_col(t):
-        tt(v("cf", 8 * t, 8 * t + 8), v("r", 8 * t, 8 * t + 8), v("b4", 0, 8), A.add)
-        cp(v("co", 8 * t, 8 * t + 8), v("cf", 8 * t, 8 * t + 8))
+    def gone_list(t):
+        tt(v("z", 0, 128), v("p3", 256, 384), v("sm", 0, 128), A.mult)
+        scan(v("zs", 0, 128), v("rs16", 0, 128), v("z", 0, 128), A.mult, A.add)
+        cp(v("co", 8 * t, 8 * t + 8), v("zs", 15, 128, 16))
 
     for ps in range(NP):
         s0 = 6 * ps
         last = ps == NP - 1
-        full_round(s0, "rc" if ps else None)
-        for (n, a, b, o) in (("p1", 256, 512, 0), ("p2", 384, 512, 256), ("p3", 128, 256, 384)):
-            act(v("g29", o, o + b - a), v(n, a, b), F.Relu, float(2 ** 29), -float(2 ** 21))
-        gone_r(0)
-        r0 = v("r", 0, 8)
-        ts(v("sar", 0, 8), r0, 0.0, A.is_le)
-        ts(v("sar", 8, 16), r0, 2.0, A.is_le, 2.0, A.add)
-        ts(v("s1"), r0, 1.0, A.is_le, 1.0, A.add)
-        gone_col(0)
-        if ps:
-            tt(v("kb"), v("g29"), v("rc"), A.add)
-        tt(v("sac"), v("sar"), v("b4"), A.add)
-        tt(v("dd", 0, 8), v("s1"), v("sar", 0, 8), A.subtract)
-        tt(v("dd", 8, 16), v("s1"), v("sar", 8, 16), A.subtract)
+        if ps == 0:
+            late_loads()
+        full_round(s0, ["rc"] if ps else [])
+        gone("x0", 0)
         ms(own(s0 + 3), K)
         if ps == 0:
             late_consts()
-        full_round(s0 + 1, "kb" if ps else "g29")
-        gone_r(1)
-        tt(v("ee", 0, 8), v("r", 8, 16), v("sar", 0, 8), A.is_equal)
-        tt(v("ee", 8, 16), v("r", 8, 16), v("sar", 8, 16), A.is_equal)
-        tt(v("ff"), v("ee"), v("dd"), A.mult)
-        tt(v("lhf"), v("ff"), v("sac"), A.add)
-        cp(v("lh"), v("lhf"))
-        cp(v("tsel"), ind(v("trii"), v("lh")))
+        gone_list(0)
+        full_round(s0 + 1, ["x0", "rc"] if ps else ["x0"])
+
+        def left_a(h):
+            act(v("yy", 256 * h, 256 * h + 256), PD(h), F.Abs, -1.5, 1.0 / 256)
+            b = "p%d" % (2 + h)
+            mm(v(b, 0, 128), "i1", v("c25"), True)
+            for e, (r2, r1) in enumerate(((0, 1), (3, 2))):
+                mm(v(b, 64 * e, 64 * e + 64), "i2", v("yy", 256 * h + r2, 256 * h + 256, 4))
+                mm(v(b, 64 * e, 64 * e + 64), "i1", v("yy", 256 * h + r1, 256 * h + 256, 4), False, e == 1)
+
+        def left_b(h):
+            a = 128 * h
+            return [
+                lambda: tt(v("zb", a, a + 128), v("p%d" % (2 + h), 0, 128), v("sm", 0, 128), A.mult),
+                lambda: scan(v("zsb", a, a + 128), v("rs16", 0, 128), v("zb", a, a + 128), A.mult, A.max),
+                lambda: (tt(v("lhf", 8 * h, 8 * h + 4), v("zsb", a + 15, a + 64, 16), v("b4", 4 * h, 4 * h + 4), A.add),
+                         tt(v("lhf", 8 * h + 4, 8 * h + 8), v("b4", 8 + 4 * h, 12 + 4 * h), v("zsb", a + 79, a + 128, 16), A.subtract)),
+                lambda: cp(v("lh", 8 * h, 8 * h + 8), v("lhf", 8 * h, 8 * h + 8)),
+                lambda: cp(v("tsel", a, a + 128), ind(v("trii"), v("lh", 8 * h, 8 * h + 8))),
+            ]
+
+        def left_c(h):
+            a = 128 * h
+            b = "p%d" % (4 * h)
+            for j, (l0, l1) in enumerate((("pa0", "pa1"), ("pb0", "pb1"))):
+                o = v(b, 64 * j, 64 * j + 64)
+                mm(o, l0, v("tsel", a, a + 64), True)
+                mm(o, l1, v("tsel", a + 64, a + 128), False, True)
+
+        def left_d(h):
+            cp(v("ab2", 128 * h, 128 * h + 128), v("p%d" % (4 * h), 0, 128))
+
+        left_a(0)
+        left_a(1)
+        la, lb_ = left_b(0), left_b(1)
+        for f in (la[0], la[1], la[2], lb_[0], la[3], lb_[1], la[4], lb_[2]):
+            f()
+        left_c(0)
+        lb_[3]()
+        left_d(0)
+        lb_[4]()
+        left_c(1)
         act(v("psel"), ind(v("phib"), v("lh")), F.Copy)
         if ps:
-            act(v("ksel"), ind(v("rc"), v("lh")), F.Copy)
-        for j, (l0, l1) in enumerate((("pb0", "pb1"), ("pa0", "pa1"))):
-            o = v("p%d" % (6 + j), 0, 128)
-            mm(o, l0, v("tsel", 0, 128), True)
-            mm(o, l1, v("tsel", 128, 256), False, True)
-        gone_col(1)
-        tt(v("dl"), v("lhf", 0, 8), v("lhf", 8, 16), A.subtract)
-        cp(v("ab2", 128, 256), v("p6", 0, 128))
-        cp(v("ab2", 0, 128), v("p7", 0, 128))
+            act(v("ksel"), ind(v("rc"), v("lh")), F.Identity, 0.0, float(2 ** 21))
+        left_d(1)
+        gone("x1", 1)
         s = s0 + 2
         arrive(s)
 
         def bias2(h):
             if ps:
-                mm(v("p%d" % h, 0, 64), "i1", v("ksel", 64 * h, 64 * h + 64), True)
-                mm(v("p%d" % h, 0, 64), "ni", v("ksel", 128 + 64 * h, 192 + 64 * h))
+                mm(v("p%d" % h, 0, 64), "i1", v("ksel", 128 * h, 128 * h + 64), True)
+                mm(v("p%d" % h, 0, 64), "ni", v("ksel", 128 * h + 64, 128 * h + 128))
+
+        def gat2(h, c0, c1):
+            a, b, o = 128 * h + c0, 128 * h + c1, 1024 * h
+            k = c0
+            if h == 0 and c0 == 0:
+                k = c1 // 2
+                cp(v("gb", 0, 16 * k), ind(tab(s), v("ab2", 64, 64 + k)))
+            act(v("gb", o + 16 * k, o + 16 * c1), ind(tab(s), v("ab2", 128 * h + 64 + k, b + 64)), F.Copy)
+            tt(v("mn", o + 16 * c0, o + 16 * c1), ind(tab(s), v("ab2", a, b)), v("gb", o + 16 * c0, o + 16 * c1), A.min)
 
         def pe2(h):
             for j in range(16):
                 mm(v("p%d" % h, 0, 64), "ng" if j % 2 else "g1", v("mn", 1024 * h + j, 1024 * h + 1024, 16), j == 0 and ps == 0, j == 15)
 
-        def post2(h):
+        def post2a(h):
             for e, op in ((0, A.is_le), (1, A.is_gt)):
-                ts(v("sk", 128 * e + 64 * h, 128 * e + 64 * h + 64), v("p%d" % h, 0, 64), 0.0, op, K, A.mult)
-            for e in range(2):
-                a = 128 * e + 64 * h
-                tt(ind(own(s + 1), v("lh", 8 * e + 4 * h, 8 * e + 4 * h + 4)), v("psel", a, a + 64), v("sk", a, a + 64), A.add)
+                ts(v("sk", 128 * h + 64 * e, 128 * h + 64 * e + 64), v("p%d" % h, 0, 64), 0.0, op, K, A.mult)
+
+        def post2b(h):
+            a = 128 * h
+            tt(ind(own(s + 1), v("lh", 8 * h, 8 * h + 8)), v("psel", a, a + 128), v("sk", a, a + 128), A.add)
 
         bias2(0)
         bias2(1)
-        gat(s, "ab2", 128, 0, 32)
-        gat(s, "ab2", 128, 32, 64)
+        gat2(0, 0, 32)
+        gat2(0, 32, 64)
         pe2(0)
-        gat(s, "ab2", 128, 64, 96)
-        gat(s, "ab2", 128, 96, 128)
+        gat2(1, 0, 32)
+        post2a(0)
+        gat2(1, 32, 64)
         pe2(1)
-        post2(0)
-        post2(1)
+        post2b(0)
+        post2a(1)
+        post2b(1)
         send(s + 1)
-        pick_a(v("sk", 0, 128))
-        pick_b()
-        tt(v("ff", 0, 8), v("zs", 15, 128, 16), v("dl"), A.mult)
-        ts(v("ff", 0, 8), v("ff", 0, 8), 32.0 / K, A.mult)
-        tt(v("cf", 16, 24), v("ff", 0, 8), v("lhf", 8, 16), A.add)
-        cp(v("co", 16, 24), v("cf", 16, 24))
+        tt(v("zb"), v("sk"), v("sm"), A.mult)
+        if ps == 0:
+            later_consts()
+        scan(v("zsb"), v("rs16"), v("zb"), A.mult, A.add)
+        tt(v("ff"), v("zsb", 15, 256, 16), v("lhf"), A.mult)
+        for h in range(2):
+            tt(v("cf", 4 * h, 4 * h + 4), v("ff", 8 * h, 8 * h + 4), v("ff", 8 * h + 4, 8 * h + 8), A.add)
+        ts(v("co", 16, 24), v("cf"), 1.0 / K, A.mult)
         lists(2)
-        level_prep(2)
+        level_prep(2, True)
+        level_open(2, True)
         cp(own(s + 2), own(s + 1))
-        lists(1)
+        gone_list(1)
         if ps == 0:
             ms(v("al"), 1.0)
         if last:
@@ -425,60 +533,76 @@ def rank_program(g, core, T, topo):
             arrive(s)
             E = lambda j: v("p%d" % (4 + j), 0, 256)
             H = lambda n, j, k=1: v(n, 256 * j, 256 * (j + k))
-            if phase:
-                mm(v("p0", 0, 64), "i64", v("cs", 128 * t, 128 * t + 64), True)
-            for j in range(4):
-                o, a = v("gb", 512 * j, 512 * j + 512), ind(tab(s), v("ll", 128 * t + 32 * j, 128 * t + 32 * j + 32))
-                if j % 2:
-                    act(o, a, F.Copy)
-                else:
-                    cp(o, a)
+            for h in range(2):
                 for u in range(2):
-                    mm(E(j), "i1", v("gb", 512 * j + u, 512 * j + 512, 2), False, u == 1)
-
-            def sums(b, h, l, src, start, stop):
+                    j = 2 * h + u
+                    o, a = v("gb", 512 * j, 512 * j + 512), ind(tab(s), v("ll", 128 * t + 32 * j, 128 * t + 32 * j + 32))
+                    if u:
+                        act(o, a, F.Copy)
+                    else:
+                        cp(o, a)
                 for m in range(8):
-                    mm(v(b, 64 * h, 64 * h + 64), l, v(src, 512 * h + m, 512 * h + 512, 8), start and m == 0, stop and m == 7)
+                    for u in range(2):
+                        mm(v("p%d" % (4 + 2 * h + m // 4), 64 * (m % 4), 64 * (m % 4) + 64), "i1",
+                           v("gb", 1024 * h + 2 * m + u, 1024 * h + 1024, 16), False, m % 4 == 3 and u == 1)
+
+            def sums(b, j, l, src, stop=False):
+                for m in range(4):
+                    mm(v(b, 64 * (j // 2), 64 * (j // 2) + 64), l, v(src, 256 * j + 64 * m, 256 * j + 64 * m + 64), False, stop and m == 3)
+
+            def flags(j):
+                for x in range(4 * j, 4 * j + 4):
+                    mm(v("p2", 0, 64), v("zz", 16 - x, 144 - x), v("q", 64 * x, 64 * x + 64), x == 0, x == 15)
 
             ts(H("q", 0), E(0), 0.5, A.add)
             for j in (1, 2, 3):
                 act(H("q", j), E(j), F.Identity, 0.5)
-            for h in range(2):
-                for j in (2 * h, 2 * h + 1):
-                    tt(H("dw", j), E(j), H("q", j), A.subtract)
-                    if h:
-                        act(H("aw", j), H("dw", j), F.Abs)
-                if h == 0:
-                    act(H("aw", 0, 2), H("dw", 0, 2), F.Abs)
-                ts(H("vv", 2 * h, 2), H("q", 2 * h, 2), float(2 ** 20), A.is_lt)
+            for j in range(4):
+                flags(j)
+                tt(H("dw", j), E(j), H("q", j), A.subtract)
                 if phase:
-                    if h:
-                        mm(v("p0", 64, 128), "i64", v("cs", 128 * t + 64, 128 * t + 128), True)
-                    sums("p0", h, "s8", "dw", False, True)
-                sums("p1", h, "thm", "vv", True, False)
-                sums("p1", h, "g1", "aw", False, True)
-            X = v("p1", 0, 128)
-            if phase:
-                cp(v("wi"), v("p0", 0, 128))
-                ts(v("pi"), v("wi"), 6, A.arith_shift_right, 255, A.bitwise_and)
+                    sums("p0", j, "s8", "dw")
+                if j == 3 and phase:
+                    mm(v("p0", 0, 128), "i1", v("cm2"))
+                    mm(v("p0", 0, 128), "ni", v("cm2"), False, True)
+                if j >= 2:
+                    sums("p1", j, "ng", "dw")
+            for j in range(2):
+                act(H("aw", j), H("dw", j), F.Abs)
+            ts(v("vc"), v("p2", 0, 64), float(2 ** 20), A.is_lt)
+            ts(H("aw", 2, 2), H("dw", 2, 2), 0.0, A.max)
+            sums("p1", 0, "g1", "aw")
+            for h in range(2):
+                for u in range(2):
+                    mm(v("p1", 64 * h, 64 * h + 64), wt("thm", 2 * h + u), v("vc"))
+            sums("p1", 1, "g1", "aw")
+            sums("p1", 2, "g2", "aw")
+            sums("p1", 3, "g2", "aw", True)
+            X, P = v("p1", 0, 128), v("p0", 0, 128)
             if t > 0:
-                cp(v("pb"), v("pi"))
+                ts(v("pq"), P, M8, A.add, M8, A.subtract)
+                tt(v("pb"), P, v("pq"), A.subtract)
                 ts(v("rk"), X, 0.0, A.is_gt, K, A.mult)
                 tt(ind(own(s + 1), col), v("pb"), v("rk"), A.add)
                 send(s + 1)
-                level_prep(t - 1)
+                if t == 2:
+                    lists(1)
+                level_prep(t - 1, last or t > 1)
                 if t == 2:
                     cp(own(s + 2), own(s + 1))
                     lists(0)
             if last:
                 if t == 2:
                     cp(v("csf"), cs)
+                cp(v("wi"), P)
+                ts(v("pi"), v("wi"), 255, A.bitwise_and)
                 tt(v("pd"), v("pi"), cs, A.subtract)
-                ts(v("p2", 0, 128), X, 0.0, A.is_le)
-                tt(v("pt"), v("p2", 0, 128), v("pd"), A.mult)
+                ts(v("p3", 0, 128), X, 0.0, A.is_le)
+                tt(v("pt"), v("p3", 0, 128), v("pd"), A.mult)
                 tt(ind(v("yp"), col), v("pt"), v("csf"), A.add)
                 if t > 0:
                     cp(v("csf"), v("cs", 128 * t - 128, 128 * t))
+                    level_open(t - 1, True)
                 if t == 2:
                     ms(v("lev"), 3.0)
                     for u in range(3):
@@ -495,6 +619,8 @@ def rank_program(g, core, T, topo):
                 if t == 0:
                     tt(ind(own(s + 1), col), v("ams"), v("kp"), A.mult)
                     send(s + 1)
+                else:
+                    level_open(t - 1, t > 1)
                 cp(v("als"), ind(v("al"), col))
                 tt(ind(v("al"), col), v("als"), v("kp"), A.mult)
                 if t == 1:
@@ -502,7 +628,7 @@ def rank_program(g, core, T, topo):
                     cp(v("ams"), ind(own(s + 2), v("co", 0, 8)))
                 if t == 2 and ps == 0:
                     for r in range(4):
-                        ms(v("pk", r, V, 4), float((4 - r) * 2 ** 26))
+                        ms(v("pk", r, V, 4), (4 - r) / 16.0)
                 if t == 0:
                     ts(v("kb"), v("al"), -1.0, A.add)
                     tt(v("rc"), v("kb"), v("pk"), A.mult)

@@ -12,23 +12,24 @@ PAIRS = [(0, 1), (0, 2), (0, 3), (1, 2), (1, 3), (2, 3)]
 
 bf, f32, i32, u16, f16 = "bfloat16", "float32", "int32", "uint16", "float16"
 SB = {
-    "tb": (NS * W, bf), "ampi": (V, i32), "phii": (V, i32), "trii": (V, i32), "thi": (1, i32),
+    "tb": (NS * W, bf), "ampi": (V, i32), "phii": (V, i32), "trii": (V, i32), "thi": (1, i32), "tq": (V, i32),
     "tB": (V, i32), "tC": (V, f32), "tD": (V, f32), "li": (64, i32), "lu": (64, u16),
     "ab": (V, u16), "ab2": (256, u16), "phib": (V, bf), "gb": (4096, bf), "mn": (4096, bf),
-    "di": (144, i32), "gi": (128, i32), "ti": (128, i32), "gg": (24, i32), "pc": (8, i32), "pf": (16, f32), "c64": (8, f32),
+    "di": (130, i32), "zero": (V, bf), "ti": (128, i32), "gg": (24, i32), "pc": (8, i32), "pf": (16, f32), "c64": (8, f32),
     "i1": (128, bf), "ie": (128, bf), "i2": (128, bf), "i3": (128, bf), "i4": (128, bf), "ni": (128, bf), "s8": (128, bf),
-    "g1": (128, bf), "g2": (128, bf), "ng": (128, bf), "thm": (V, bf), "zz": (144, bf), "sm": (256, bf), "brow": (128, bf),
-    "lt": (V, bf), "lb": (V, bf), "eu": (V, bf), "ed": (V, bf),
-    "pa0": (128, f16), "pa1": (128, f16), "pb0": (128, f16), "pb1": (128, f16),
-    "cb": (256, bf), "cb2": (128, bf), "c25": (128, bf), "cd": (64, bf), "cm": (64, bf), "cm2": (128, bf), "cap": (1, f32),
-    "c49": (256, bf), "r256": (256, bf), "pk": (V, bf), "rs16": (256, bf), "thb": (2, bf), "thw": (4, i32),
-    "b4": (16, f32), "lc": (384, f32),
-    "cl": (128, bf), "t1": (V, i32), "t2": (V, bf), "x0": (V, bf), "x1": (V, bf), "yy": (V, bf), "kb": (V, bf), "rc": (V, bf), "al": (V, bf),
-    "z": (256, f32), "zs": (256, f32), "zb": (256, bf), "zsb": (256, bf), "ff": (16, f32), "lhf": (16, f32), "lh": (16, u16),
+    "g1": (128, bf), "g2": (128, bf), "ng": (128, bf), "thm": (V, bf), "zz": (144, bf), "zq": (144, bf), "sm": (256, bf),
+    "brow": (128, bf), "nlt": (V, bf), "nie": (128, bf), "rr": (256, bf), "lt": (V, bf), "lb": (V, bf), "eu": (V, bf),
+    "ed": (V, bf), "lv": (384, bf),
+    "pa0": (128, f16), "pa1": (128, f16), "pb0": (128, f16), "pb1": (128, f16), "i16": (128, f16),
+    "cb": (256, bf), "cb2": (128, bf), "c25": (128, bf), "cd": (64, bf), "cm": (64, bf), "c128": (128, bf), "cap": (1, f32),
+    "c49": (256, bf), "r256": (256, bf), "rs16": (256, bf), "thb": (2, bf), "thw": (4, i32), "b4": (16, f32),
+    "cl": (128, bf), "t1": (V, i32), "t2": (V, bf), "x0": (V, bf), "x1": (V, bf), "yy": (V, bf), "rc": (V, bf), "al": (V, bf),
+    "z": (128, f32), "zs": (128, f32), "zb": (256, bf), "zsb": (256, bf), "ff": (16, f32), "lhf": (16, f32), "lh": (16, u16),
     "cf": (8, f32), "co": (24, u16), "tsel": (256, f16), "ksel": (256, bf), "psel": (256, bf), "sk": (256, bf),
-    "ll": (384, u16), "cs": (384, bf), "csf": (128, f32), "q": (1024, bf), "dw": (1024, bf), "aw": (1024, bf),
-    "vc": (64, bf), "wi": (128, i32), "pi": (128, i32), "pq": (128, bf), "pb": (128, bf), "rk": (128, bf),
-    "kp": (128, bf), "als": (128, bf), "ams": (128, bf), "pd": (128, f32), "pt": (128, f32), "yp": (V, f32), "lev": (V, f32),
+    "ll": (384, u16), "lf": (256, f32), "lq": (256, f16), "lz": (128, f32), "lr": (256, u16),
+    "cs": (384, bf), "csf": (384, f32), "q": (1024, bf), "dw": (1024, bf), "aw": (1024, bf),
+    "vc": (64, bf), "pi": (128, i32), "pq": (128, bf), "pb": (128, i32), "rk": (128, bf), "kp": (384, bf),
+    "asel": (384, bf), "alsel": (384, bf), "pd": (128, bf), "pt": (128, f32), "yp": (V, f32), "lev": (V, f32),
 }
 SCRATCH = {n: ("sbuf", [128, w], d) for n, (w, d) in SB.items()}
 for _b in range(8):
@@ -147,7 +148,13 @@ def rank_program(g, core, T, topo):
         if bias is None:
             rec("S", "S", lambda: g.scalar.activation(ap(o), ap(a), func), [a], [o], take("S"))
         else:
-            rec("S", "S", lambda: g.scalar.activation(ap(o), ap(a), func, bias=bias, scale=ap(scale)), [a, scale], [o], take("S"))
+            rec("S", "S", lambda: g.scalar.activation(ap(o), ap(a), func, bias=ap(bias), scale=ap(scale)), [a, bias, scale], [o], take("S"))
+
+    def const(o, c):
+        act(o, v("zero", 0, (o[2] - o[1] + o[3] - 1) // o[3]), F.Identity, c)
+
+    def times(o, a, c):
+        act(o, a, F.Identity, 0.0, c)
 
     def mm(o, l, r, start=False, stop=False):
         l = v(l) if isinstance(l, str) else l
@@ -159,11 +166,14 @@ def rank_program(g, core, T, topo):
         else:
             rec("G", "G", lambda: g.iota(ap(o), pat, base, cm), [], [o])
 
+    def aff(o, a, pat, op, fill, base, cm):
+        rec("G", "G", lambda: g.affine_select(ap(o), ap(a), pat, op, fill, base, cm), [a], [o])
+
     ndma = {d: 0 for d in DMAS}
 
-    def dma(q, name, o, a, reads, writes, extra=()):
+    def dma(q, name, o, a, reads, writes):
         ndma[name] += 1
-        rec(q, "d_" + name, lambda: Q[q].dma_start(o, a), reads, writes, extra)
+        rec(q, "d_" + name, lambda: Q[q].dma_start(o, a), reads, writes)
 
     peers = [c for c in T.cores if c != core]
     far = [c for c in peers if topo.chip(c) != topo.chip(core)]
@@ -181,8 +191,12 @@ def rank_program(g, core, T, topo):
     def tab(s):
         return v("tb", s * W, (s + 1) * W)
 
-    def send(s, a=0, b=V):
-        x = own(s, a, b)
+    def new(s0, t):
+        a = (s0 + 4) * W + (0 if t == 2 else V + 16) + 128 * rank
+        return v("tb", a, a + 128)
+
+    def send(s, a=0, b=V, x=None):
+        x = x or own(s, a, b)
         nsend[s] += 1
 
         def call():
@@ -204,36 +218,47 @@ def rank_program(g, core, T, topo):
         a, e = c // 2, c % 2
         dma("YS"[e], "la", T.tB[32 * a:32 * a + 32, 256 * e:256 * e + 256], T.tri[16 * c:16 * c + 16, :], [],
             [v("tB", 256 * e + a, 256 * e + 256, 4)])
-    iota(v("di"), [[1, 144]], 128, -1)
+    dma("Y", "th", T.thi[:], T.th[:], [], [v("thi")])
+    dma("S", "phi", T.phii[:], T.phi[:], [], [v("phii")])
+    dma("Y", "tri", T.trii[:], T.tri[:], [], [v("trii")])
     iota(v("pc", 0, 1), [[1, 1]], 0, 1)
+    iota(v("di"), [[1, 130]], 128, -1)
     iota(v("gg"), [[0, 3], [16, 8]], 15, -1)
     iota(v("li", 0, 32), [[16, 16], [256, 2]], 0, 0)
     iota(v("li", 32, 64), [[2, 2], [1, 2], [4, 8]], 0, 0)
-    iota(v("gi"), [[16, 8], [0, 16]], 15, -1)
     iota(v("c64"), [[64, 8]], 0, 0, True)
     d128 = v("di", 0, 128)
-    ms(v("cb"), -31.0 / 64)
+    ms(v("zero"), 0.0)
     ms(v("lt"), 0.0)
     ms(v("cd"), -31.0 / 64)
     ms(v("cm"), M1)
     ms(v("cap"), 255.0)
-    for r in range(4):
-        ms(v("r256", r, 256, 4), 256.0 * r)
+    ts(v("pc", 1, 2), v("pc", 0, 1), 15, A.bitwise_and)
     ms_hi("cd", -1.0)
     ms_hi("cm", 0.0)
     ms_hi("cap", 1.0)
-    ts(v("ti"), d128, 15, A.bitwise_and)
-    ts(v("pc", 1, 2), v("pc", 0, 1), 15, A.bitwise_and)
-    ts(v("gg"), v("gg"), 4, A.arith_shift_right)
     ts(v("i1"), d128, 128.0, A.is_equal)
+    ts(v("ti"), d128, 15, A.bitwise_and)
+    ts(v("gg"), v("gg"), 4, A.arith_shift_right)
     cp(v("pf", 0, 1), v("pc", 1, 2))
     ts(v("pf", 1, 2), v("pc", 1, 2), 32.0, A.mult)
-    ts(v("ie"), d128, 128.0, A.is_equal, 0.125, A.mult)
-    ts(v("ni"), d128, 128.0, A.is_equal, -1.0, A.mult)
+    ts(v("pf", 2, 3), v("pc", 0, 1), 64.0, A.is_lt, 32.0, A.mult)
+    ts(v("pf", 3, 4), v("pc", 0, 1), 64.0, A.is_ge, 128.0, A.mult)
+    ts(v("lu", 0, 32), v("li", 0, 32), v("pf", 0, 1), A.add)
     cp(own(0), v("ampi"))
     send(0)
+    const(v("cb"), -31.0 / 64)
+    for r in range(4):
+        const(v("r256", r, 256, 4), 256.0 * r)
+    times(v("ie"), v("i1"), 0.125)
+    times(v("ni"), v("i1"), -1.0)
+    const(v("lb"), 0.0)
+    const(v("rs16"), 1.0)
+    const(v("rs16", 0, 256, 16), 0.0)
     iota(v("brow"), [[1, 128]], 0, 0, True)
-    ts(v("lu", 0, 32), v("li", 0, 32), v("pf", 0, 1), A.add)
+    iota(v("g2"), [[0, 128]], 1, 0, True)
+    aff(v("ng"), v("g2"), [[-16, 8], [0, 16]], A.is_ge, 0.0, 0, 1)
+    aff(v("g1"), v("ng"), [[16, 8], [0, 16]], A.is_ge, 0.0, 15, -1)
     ts(v("lu", 32, 64), v("li", 32, 64), v("pf", 1, 2), A.add)
     for r in range(4):
         ts(v("lt", 144 * r, 144 * r + 16), v("ti", 0, 16), 0.0, A.is_equal, 1.0 / 32, A.mult)
@@ -246,78 +271,98 @@ def rank_program(g, core, T, topo):
                 runs.append([q, q + 1, sg])
         for q0, q1, sg in runs:
             ts(v("lt", 128 * r + 64 + 8 * q0, 128 * r + 64 + 8 * q1), v("gg", 0, 8 * (q1 - q0)), 0.0, A.is_equal, sg, A.mult)
-    ts(v("pf", 2, 3), v("pc", 0, 1), 64.0, A.is_lt, 32.0, A.mult)
-    ts(v("pf", 3, 4), v("pc", 0, 1), 64.0, A.is_ge, 128.0, A.mult)
     for r in range(4):
         mm(v("p7", 128 * r, 128 * r + 128), v("lt", 128 * r, 128 * r + 128), v("i1"), True, True)
-    act(v("eu"), v("p7"), F.Identity, 0.0, v("pf", 2, 3))
-    act(v("ed"), v("p7"), F.Identity, 0.0, v("pf", 3, 4))
+    times(v("eu"), v("p7"), v("pf", 2, 3))
+    times(v("ed"), v("p7"), v("pf", 3, 4))
     cp(v("tC"), ind(v("tB"), v("lu", 0, 32)))
     rec("V", "V", lambda: g.vector.transpose(T.tD[:], T.tC[:]), [v("tC")], [v("tD")])
     cp(v("ab"), ind(v("tD"), v("lu", 32, 64)))
     ts(v("sm", 0, 128), v("ti"), 0.0, A.is_equal)
-    ts(v("sm", 128, 256), v("ti"), 0.0, A.is_equal)
-    ms(v("rs16"), 1.0)
-    ts(v("i2"), d128, 128.0, A.is_equal, 2.0, A.mult)
-    ms(v("rs16", 0, 256, 16), 0.0)
-    ts(v("i3"), d128, 128.0, A.is_equal, 3.0, A.mult)
-    ts(v("i4"), d128, 128.0, A.is_equal, 4.0, A.mult)
-    ms(v("lb"), 0.0)
+    ts(v("pc", 2, 3), v("pc", 0, 1), 1, A.bitwise_and)
+    ts(v("pf", 4, 5), v("pc", 1, 2), 4.0, A.mult)
+    ts(v("pf", 15, 16), v("pc", 1, 2), 4.0, A.mult, 3.0, A.add)
+    ts(v("pf", 14, 15), v("pc", 1, 2), 0.0, A.is_equal)
+    cp(v("pf", 7, 8), v("thi"))
+    cp(v("pf", 5, 6), v("pc", 2, 3))
+    ts(v("pf", 6, 7), v("pc", 2, 3), 0.0, A.is_equal)
+    ts(v("tq"), v("trii"), 2, A.arith_shift_right)
+    cp(v("phib"), v("phii"))
+    times(v("nlt"), v("lt"), -1.0)
+    times(v("nie"), v("i1"), -0.125)
     for r in range(4):
-        act(v("lb", 128 * r + 64, 128 * r + 112), v("lt", 128 * r + 64, 128 * r + 112), F.Identity, 0.0, 65536.0)
+        times(v("lb", 128 * r + 64, 128 * r + 112), v("lt", 128 * r + 64, 128 * r + 112), 65536.0)
+    for r in (2, 3, 4):
+        times(v("i%d" % r), v("i1"), float(r))
 
-    def late_loads():
-        x = [("arr0", nsend[0] * per_arr)]
-        dma("Y", "tri", T.trii[:], T.tri[:], [], [v("trii")], x)
-        dma("Y", "phi", T.phii[:], T.phi[:], [], [v("phii")])
-        dma("Y", "th", T.thi[:], T.th[:], [], [v("thi")])
-
-    def late_consts():
-        ts(v("gi"), v("gi"), 4, A.arith_shift_right)
-        ts(v("pc", 2, 3), v("pc", 0, 1), 1, A.bitwise_and)
-        ts(v("pf", 4, 5), v("pc", 1, 2), 4.0, A.mult)
-        cp(v("pf", 7, 8), v("thi"))
-        ts(v("g1"), v("gi"), 0.0, A.is_equal)
-        cp(v("pf", 5, 6), v("pc", 2, 3))
-        ts(v("pf", 6, 7), v("pc", 2, 3), 0.0, A.is_equal)
-        ts(v("thb"), v("c64", 0, 2), 0.0, A.mult, v("pf", 7, 8), A.add)
-        ts(v("b4", 0, 8), v("c64"), v("pf", 4, 5), A.add)
-        ts(v("b4", 8, 16), v("c64"), v("pf", 4, 5), A.add, 3.0, A.add)
+    def consts0():
+        const(v("thb"), v("pf", 7, 8))
         mm(v("p5", 256, 258), "g1", v("thb"), True, True)
+        act(v("b4", 0, 8), v("c64"), F.Identity, v("pf", 4, 5))
+        act(v("b4", 8, 16), v("c64"), F.Identity, v("pf", 15, 16))
+        const(v("c25"), -2.5)
+        times(v("ng"), v("g1"), -1.0)
+        times(v("pq"), v("sm", 0, 128), 1.0 / 64)
+        const(v("zq"), v("pf", 14, 15))
+
+    def consts1():
+        aff(v("s8"), v("pq"), [[1, 128]], A.not_equal, 9.0 / 64, 0, -1)
+        aff(v("zz"), v("zq"), [[1, 144]], A.is_equal, 0.0, -16, -1)
+        cp(v("thw", 0, 2), v("p5", 256, 258))
         ts(v("pa0"), d128, 128.0, A.is_equal, v("pf", 6, 7), A.mult)
         ts(v("pa1"), d128, 129.0, A.is_equal, v("pf", 6, 7), A.mult)
-        ts(v("pb0"), d128, 127.0, A.is_equal, v("pf", 5, 6), A.mult)
-        ts(v("pb1"), d128, 128.0, A.is_equal, v("pf", 5, 6), A.mult)
-        cp(v("thw", 0, 2), v("p5", 256, 258))
-        ms(v("c25"), -2.5)
-        act(v("ng"), v("g1"), F.Identity, 0.0, -1.0)
-        cp(v("phib"), v("phii"))
-
-    def later_consts():
         ts(v("thw", 2, 3), v("thw", 0, 1), 4, A.arith_shift_right)
         ts(v("thw", 3, 4), v("thw", 0, 1), 15, A.bitwise_and)
+        ts(v("pb0"), d128, 127.0, A.is_equal, v("pf", 5, 6), A.mult)
+        ts(v("pb1"), d128, 128.0, A.is_equal, v("pf", 5, 6), A.mult)
         ts(v("pf", 8, 9), v("pc", 1, 2), 8.0, A.is_lt)
         ts(v("pf", 9, 10), v("pc", 1, 2), 8.0, A.is_ge)
-        ts(v("pf", 14, 15), v("pc", 1, 2), 0.0, A.is_equal)
         for h in range(2):
             ts(v("pf", 10 + 2 * h, 11 + 2 * h), v("thw", 2, 3), -16.0, A.mult, v("pf", 8 + h, 9 + h), A.mult)
             ts(v("pf", 11 + 2 * h, 12 + 2 * h), v("thw", 3, 4), -1.0, A.mult, v("pf", 8 + h, 9 + h), A.mult)
-        ts(v("zz"), v("di"), 144.0, A.is_equal, v("pf", 14, 15), A.mult)
+        times(v("sm", 128, 256), v("sm", 0, 128), 1.0)
+        const(v("c49"), 49152.0)
+        const(v("cb2"), -63.0 / 128)
+        times(v("zq"), v("zz"), 528.0 / K)
+
+    def consts2():
         for u in range(4):
-            act(v("thm", 128 * u, 128 * u + 128), v("g1"), F.Identity, 0.0, v("pf", 10 + u, 11 + u))
-        act(v("g2"), v("g1"), F.Identity, 0.0, 2.0)
-        ts(v("s8"), v("ti"), 0.0, A.is_equal, 1.0 / 64, A.mult)
-        ms(v("c49"), 49152.0)
-        ms(v("cb2"), -63.0 / 128)
-        ms(v("cm2"), M1)
-        tt(v("s8"), v("s8"), v("ie"), A.add)
+            times(v("thm", 128 * u, 128 * u + 128), v("g1"), v("pf", 10 + u, 11 + u))
+        times(v("g2"), v("g1"), 2.0)
+        const(v("c128"), -128.0)
+
+    def sel(n, src, t, k=1):
+        act(v(n, 128 * t, 128 * (t + k)), ind(src, v("co", 8 * t, 8 * (t + k))), F.Copy)
 
     def lists(t):
-        cp(v("cs", 128 * t, 128 * t + 128), ind(v("phib"), v("co", 8 * t, 8 * t + 8)))
         cp(v("ll", 128 * t, 128 * t + 128), ind(v("trii"), v("co", 8 * t, 8 * t + 8)))
 
-    def level_prep(t, phase):
-        for j in range(4):
+    def lists_x(t, part=None):
+        col = v("co", 8 * t, 8 * t + 8)
+        if part != 1:
+            cp(v("lf", 128 * t, 128 * t + 128), ind(v("trii"), col))
+        if part != 0:
+            ts(v("lq", 128 * t, 128 * t + 128), ind(v("tq"), col), -1664.0, A.add)
+
+    def redirect_a(s0, t):
+        G = lambda a, b: (v("gb", 16 * a, 16 * b), ind(tab(s0 + 3), v("ll", 128 * t + a, 128 * t + b)))
+        act(*G(0, 64), F.Copy)
+        cp(*G(64, 96))
+        act(*G(96, 128), F.Copy)
+
+    def redirect_p(t, h):
+        if h == 0:
+            mm(v("p3", 384, 512), "i16", v("lq", 128 * t, 128 * t + 128), True)
+            mm(v("p3", 384, 512), "i4", v("c128"))
+        for x in range(16):
+            mm(v("p3", 384 + 64 * h, 448 + 64 * h), v("zq", 16 - x, 144 - x), v("gb", 1024 * h + x, 1024 * h + 1024, 16), False, h == 1 and x == 15)
+
+    def redirect_b(t):
+        tt(v("lz"), v("p3", 384, 512), v("lf", 128 * t, 128 * t + 128), A.max)
+        ts(v("lr", 128 * t, 128 * t + 128), v("lz"), float(W + V if t else 4 * W), A.min)
+
+    def level_prep(t, js=range(4)):
+        for j in js:
             mm(v("p%d" % (4 + j), 0, 256), "i1", v("c49"), True)
             for m in range(4):
                 mm(v("p%d" % (4 + j), 64 * m, 64 * m + 64), "ni", v("cs", 128 * t + 64 * (j // 2), 128 * t + 64 * (j // 2) + 64))
@@ -342,7 +387,7 @@ def rank_program(g, core, T, topo):
     PD = lambda h, r=0, st=1: v("p%d" % (6 + h), r, 256, st)
     wt = lambda n, r: v(n, 128 * r, 128 * r + 128)
 
-    def full_round(s, biases):
+    def full_round(s, biases, slack):
         for h in range(2):
             mm(PS(h), "i1", v("cb"), True)
             mm(DU(h), "i1", v("cd"), True)
@@ -352,16 +397,18 @@ def rank_program(g, core, T, topo):
         for h in range(2):
             mm(PD(h), "i1", v("r256"), True)
 
+        def add(h, x, a, l4, l1, end=False):
+            for r in range(4):
+                mm(DU(h), wt(l4, r), v(x, a + r, a + 256, 4))
+            if end:
+                mm(DU(h), "i1", v("cm"))
+                mm(DU(h), "ni", v("cm"), False, True)
+            mm(PS(h), l1, v(x, a, a + 256), False, end)
+
         def piece(h, m0, m1):
             gat(s, "ab", 256, 128 * h + 16 * m0, 128 * h + 16 * m1)
             for m in range(m0, m1):
-                a = 2048 * h + 256 * m
-                for r in range(4):
-                    mm(DU(h), wt("lt", r), v("mn", a + r, a + 256, 4))
-                if m == 7:
-                    mm(DU(h), "i1", v("cm"))
-                    mm(DU(h), "ni", v("cm"), False, True)
-                mm(PS(h), "ie", v("mn", a, a + 256), False, m == 7)
+                add(h, "mn", 2048 * h + 256 * m, "lt", "ie", m == 7)
 
         def clamp(h):
             c = v("cl", 64 * h, 64 * h + 64)
@@ -384,45 +431,83 @@ def rank_program(g, core, T, topo):
         m1(0)
         piece(1, 2, 4)
         m2(0)
-        piece(1, 4, 6)
+        gat(s, "ab", 256, 192, 224)
+        x, y = v("mn", 3840, 4096), v("gb", 3840, 4096)
+        act(y, ind(tab(s), v("ab", 496, 512)), F.Copy)
+        act(x, ind(tab(s), v("ab", 240, 256)), F.Copy)
         m3(0)
         send(s + 1, 0, 256)
-        piece(1, 6, 7)
-        piece(1, 7, 8)
+        gat(s, "ab", 256, 224, 240)
+        mm(v("p5", 256, 512), "i1", x, True)
+        mm(v("p5", 256, 512), "ni", y, False, True)
+        act(v("rr"), v("p5", 256, 512), F.Relu)
+        for m in (7, 4, 5):
+            add(1, "mn", 2048 + 256 * m, "lt", "ie")
+        add(1, "rr", 0, "nlt", "nie")
+        add(1, "mn", 2048 + 256 * 6, "lt", "ie", True)
+        slack()
         clamp(1)
         m1(1)
         m2(1)
         m3(1)
         send(s + 1, 256, 512)
 
-    def gone(x, t):
-        for h in range(2):
-            act(v(x, 256 * h, 256 * h + 256), PD(h), F.Relu, 1.0, -1.0 / 256)
+    def mark(x, h):
+        act(v(x, 256 * h, 256 * h + 256), PD(h), F.Relu, 1.0, -1.0 / 256)
+
+    def gone(x):
         o = v("p3", 256, 384)
         mm(o, "i4", v("brow"), True)
         for r in (1, 2, 3):
             mm(o, "i%d" % r, v(x, r, V, 4), False, r == 3)
 
     def gone_list(t):
-        tt(v("z", 0, 128), v("p3", 256, 384), v("sm", 0, 128), A.mult)
-        scan(v("zs", 0, 128), v("rs16", 0, 128), v("z", 0, 128), A.mult, A.add)
-        cp(v("co", 8 * t, 8 * t + 8), v("zs", 15, 128, 16))
+        return [lambda: tt(v("z"), v("p3", 256, 384), v("sm", 0, 128), A.mult),
+                lambda: scan(v("zs"), v("rs16", 0, 128), v("z"), A.mult, A.add),
+                lambda: cp(v("co", 8 * t, 8 * t + 8), v("zs", 15, 128, 16))]
 
     for ps in range(NP):
         s0 = 6 * ps
         last = ps == NP - 1
+
+        def slack0():
+            mark("x0", 0)
+            if ps == 0:
+                consts0()
+            if not last:
+                act(own(s0 + 6), own(s0), F.Copy)
+            else:
+                act(v("yp"), v("phib"), F.Copy)
+                for u, c in enumerate((-1.0 / (8 * K), -23.0 / 8, -7.0 / 8)):
+                    times(wt("lv", u), v("i1"), c)
+
+        def fill(h):
+            act(own(s0 + 3, 256 * h, 256 * h + 256), PD(h), F.Abs, 9 * K, -10 * K / 768)
+
+        def slack1():
+            act(v("yy", 0, 256), PD(0), F.Abs, -1.5, 1.0 / 256)
+            fill(0)
+            mark("x1", 0)
+            sel("cs", v("phib"), 0)
+            if not last:
+                sel("asel", own(s0), 0)
+
+        full_round(s0, ["rc"] if ps else [], slack0)
+        mark("x0", 1)
+        gone("x0")
+        ms(v("tb", (s0 + 4) * W + V, (s0 + 4) * W + V + 16), K)
         if ps == 0:
-            late_loads()
-        full_round(s0, ["rc"] if ps else [])
-        gone("x0", 0)
-        ms(own(s0 + 3), K)
-        if ps == 0:
-            late_consts()
-        gone_list(0)
-        full_round(s0 + 1, ["x0", "rc"] if ps else ["x0"])
+            consts1()
+        for f in gone_list(0):
+            f()
+        lists(0)
+        if ps:
+            lists_x(0)
+        full_round(s0 + 1, ["x0", "rc"] if ps else ["x0"], slack1)
 
         def left_a(h):
-            act(v("yy", 256 * h, 256 * h + 256), PD(h), F.Abs, -1.5, 1.0 / 256)
+            if h:
+                act(v("yy", 256, 512), PD(1), F.Abs, -1.5, 1.0 / 256)
             b = "p%d" % (2 + h)
             mm(v(b, 0, 128), "i1", v("c25"), True)
             for e, (r2, r1) in enumerate(((0, 1), (3, 2))):
@@ -451,21 +536,24 @@ def rank_program(g, core, T, topo):
         def left_d(h):
             cp(v("ab2", 128 * h, 128 * h + 128), v("p%d" % (4 * h), 0, 128))
 
+        def left_s(h):
+            a, l = 128 * h, v("lh", 8 * h, 8 * h + 8)
+            if ps:
+                times(v("ksel", a, a + 128), ind(v("rc"), l), float(2 ** 21))
+            act(v("psel", a, a + 128), ind(v("phib"), l), F.Copy)
+
         left_a(0)
         left_a(1)
         la, lb_ = left_b(0), left_b(1)
         for f in (la[0], la[1], la[2], lb_[0], la[3], lb_[1], la[4], lb_[2]):
             f()
+        left_s(0)
         left_c(0)
         lb_[3]()
         left_d(0)
         lb_[4]()
+        left_s(1)
         left_c(1)
-        act(v("psel"), ind(v("phib"), v("lh")), F.Copy)
-        if ps:
-            act(v("ksel"), ind(v("rc"), v("lh")), F.Identity, 0.0, float(2 ** 21))
-        left_d(1)
-        gone("x1", 1)
         s = s0 + 2
         arrive(s)
 
@@ -480,6 +568,7 @@ def rank_program(g, core, T, topo):
             if h == 0 and c0 == 0:
                 k = c1 // 2
                 cp(v("gb", 0, 16 * k), ind(tab(s), v("ab2", 64, 64 + k)))
+                left_d(1)
             act(v("gb", o + 16 * k, o + 16 * c1), ind(tab(s), v("ab2", 128 * h + 64 + k, b + 64)), F.Copy)
             tt(v("mn", o + 16 * c0, o + 16 * c1), ind(tab(s), v("ab2", a, b)), v("gb", o + 16 * c0, o + 16 * c1), A.min)
 
@@ -487,12 +576,10 @@ def rank_program(g, core, T, topo):
             for j in range(16):
                 mm(v("p%d" % h, 0, 64), "ng" if j % 2 else "g1", v("mn", 1024 * h + j, 1024 * h + 1024, 16), j == 0 and ps == 0, j == 15)
 
-        def post2a(h):
-            for e, op in ((0, A.is_le), (1, A.is_gt)):
-                ts(v("sk", 128 * h + 64 * e, 128 * h + 64 * e + 64), v("p%d" % h, 0, 64), 0.0, op, K, A.mult)
-
-        def post2b(h):
+        def post2(h):
             a = 128 * h
+            for e, op in ((0, A.is_le), (1, A.is_gt)):
+                ts(v("sk", a + 64 * e, a + 64 * e + 64), v("p%d" % h, 0, 64), 0.0, op, 8 * K, A.mult)
             tt(ind(own(s + 1), v("lh", 8 * h, 8 * h + 8)), v("psel", a, a + 128), v("sk", a, a + 128), A.add)
 
         bias2(0)
@@ -501,30 +588,47 @@ def rank_program(g, core, T, topo):
         gat2(0, 32, 64)
         pe2(0)
         gat2(1, 0, 32)
-        post2a(0)
         gat2(1, 32, 64)
-        pe2(1)
-        post2b(0)
-        post2a(1)
-        post2b(1)
-        send(s + 1)
-        tt(v("zb"), v("sk"), v("sm"), A.mult)
+        fill(1)
+        mark("x1", 1)
         if ps == 0:
-            later_consts()
+            consts2()
+        pe2(1)
+        post2(0)
+        post2(1)
+        send(s + 1)
+        gone("x1")
+        if last:
+            for u, x in enumerate((own(s0 + 3), v("x0"), v("x1"))):
+                mm(v("p2"), wt("lv", u), x, u == 0, u == 2)
+        gl = gone_list(1)
+        tt(v("zb"), v("sk"), v("sm"), A.mult)
+        gl[0]()
         scan(v("zsb"), v("rs16"), v("zb"), A.mult, A.add)
+        gl[1]()
         tt(v("ff"), v("zsb", 15, 256, 16), v("lhf"), A.mult)
+        gl[2]()
         for h in range(2):
             tt(v("cf", 4 * h, 4 * h + 4), v("ff", 8 * h, 8 * h + 4), v("ff", 8 * h + 4, 8 * h + 8), A.add)
-        ts(v("co", 16, 24), v("cf"), 1.0 / K, A.mult)
-        lists(2)
-        level_prep(2, True)
-        level_open(2, True)
-        cp(own(s + 2), own(s + 1))
-        gone_list(1)
+        lists(1)
+        ts(v("co", 16, 24), v("cf"), 1.0 / (8 * K), A.mult)
+        sel("cs", v("phib"), 1)
         if ps == 0:
-            ms(v("al"), 1.0)
-        if last:
-            cp(v("yp"), v("phii"))
+            ts(v("i16"), d128, 128.0, A.is_equal)
+        lists_x(1)
+        sel("cs", v("phib"), 2)
+        lists(2)
+        level_prep(2)
+        level_open(2, True)
+        if not last:
+            sel("asel", own(s0), 1, 2)
+        else:
+            act(v("csf", 256, 384), v("cs", 256, 384), F.Copy)
+            act(v("lev"), v("p2"), F.Identity, 3.0)
+            for c in range(8):
+                dma("Y", "ol", T.ylev[c:c + 1, :], T.lev[16 * c:16 * c + 1, :], [v("lev")], [])
+        if ps == 0:
+            lists_x(0, 0)
         for t in (2, 1, 0):
             s = s0 + 5 - t
             col = v("co", 8 * t, 8 * t + 8)
@@ -533,49 +637,49 @@ def rank_program(g, core, T, topo):
             arrive(s)
             E = lambda j: v("p%d" % (4 + j), 0, 256)
             H = lambda n, j, k=1: v(n, 256 * j, 256 * (j + k))
+            win = v("tb", (s0 + 3) * W, (s0 + 4) * W + (0, V + 16, 2 * V + 16)[2 - t])
+            G = lambda a, b: (v("gb", 16 * a, 16 * b), ind(win, v("lr" if t < 2 else "ll", 128 * t + a, 128 * t + b)))
             for h in range(2):
-                for u in range(2):
-                    j = 2 * h + u
-                    o, a = v("gb", 512 * j, 512 * j + 512), ind(tab(s), v("ll", 128 * t + 32 * j, 128 * t + 32 * j + 32))
-                    if u:
-                        act(o, a, F.Copy)
-                    else:
-                        cp(o, a)
+                cp(*G(64 * h, 64 * h + 32))
+                act(*G(64 * h + 32, 64 * h + 64), F.Copy)
                 for m in range(8):
                     for u in range(2):
                         mm(v("p%d" % (4 + 2 * h + m // 4), 64 * (m % 4), 64 * (m % 4) + 64), "i1",
                            v("gb", 1024 * h + 2 * m + u, 1024 * h + 1024, 16), False, m % 4 == 3 and u == 1)
 
             def sums(b, j, l, src, stop=False):
-                for m in range(4):
-                    mm(v(b, 64 * (j // 2), 64 * (j // 2) + 64), l, v(src, 256 * j + 64 * m, 256 * j + 64 * m + 64), False, stop and m == 3)
+                if b == "p1" or phase:
+                    for m in range(4):
+                        mm(v(b, 64 * (j // 2), 64 * (j // 2) + 64), l, v(src, 256 * j + 64 * m, 256 * j + 64 * m + 64), False, stop and m == 3)
 
             def flags(j):
                 for x in range(4 * j, 4 * j + 4):
                     mm(v("p2", 0, 64), v("zz", 16 - x, 144 - x), v("q", 64 * x, 64 * x + 64), x == 0, x == 15)
 
-            ts(H("q", 0), E(0), 0.5, A.add)
+            dw = lambda j: tt(H("dw", j), E(j), H("q", j), A.subtract)
             for j in (1, 2, 3):
                 act(H("q", j), E(j), F.Identity, 0.5)
-            for j in range(4):
-                flags(j)
-                tt(H("dw", j), E(j), H("q", j), A.subtract)
-                if phase:
-                    sums("p0", j, "s8", "dw")
-                if j == 3 and phase:
-                    mm(v("p0", 0, 128), "i1", v("cm2"))
-                    mm(v("p0", 0, 128), "ni", v("cm2"), False, True)
-                if j >= 2:
-                    sums("p1", j, "ng", "dw")
+            ts(H("q", 0), E(0), 0.5, A.add)
+            flags(0)
             for j in range(2):
+                dw(j)
                 act(H("aw", j), H("dw", j), F.Abs)
-            ts(v("vc"), v("p2", 0, 64), float(2 ** 20), A.is_lt)
-            ts(H("aw", 2, 2), H("dw", 2, 2), 0.0, A.max)
+                sums("p0", j, "s8", "dw")
+                flags(j + 1)
+            flags(3)
+            dw(2)
+            sums("p0", 2, "s8", "dw")
+            sums("p1", 2, "ng", "dw")
             sums("p1", 0, "g1", "aw")
+            dw(3)
+            sums("p0", 3, "s8", "dw", True)
+            sums("p1", 3, "ng", "dw")
+            ts(v("vc"), v("p2", 0, 64), float(2 ** 20), A.is_lt)
             for h in range(2):
                 for u in range(2):
                     mm(v("p1", 64 * h, 64 * h + 64), wt("thm", 2 * h + u), v("vc"))
             sums("p1", 1, "g1", "aw")
+            ts(H("aw", 2, 2), H("dw", 2, 2), 0.0, A.max)
             sums("p1", 2, "g2", "aw")
             sums("p1", 3, "g2", "aw", True)
             X, P = v("p1", 0, 128), v("p0", 0, 128)
@@ -583,55 +687,48 @@ def rank_program(g, core, T, topo):
                 ts(v("pq"), P, M8, A.add, M8, A.subtract)
                 tt(v("pb"), P, v("pq"), A.subtract)
                 ts(v("rk"), X, 0.0, A.is_gt, K, A.mult)
-                tt(ind(own(s + 1), col), v("pb"), v("rk"), A.add)
-                send(s + 1)
-                if t == 2:
-                    lists(1)
-                level_prep(t - 1, last or t > 1)
-                if t == 2:
-                    cp(own(s + 2), own(s + 1))
-                    lists(0)
+                tt(new(s0, t), v("pb"), v("rk"), A.add)
+                send(s + 1, x=new(s0, t))
+                redirect_a(s0, t - 1)
+                redirect_p(t - 1, 0)
+                level_prep(t - 1, (0,))
+                redirect_p(t - 1, 1)
+                level_prep(t - 1, (1, 2, 3))
             if last:
-                if t == 2:
-                    cp(v("csf"), cs)
-                cp(v("wi"), P)
-                ts(v("pi"), v("wi"), 255, A.bitwise_and)
+                if t == 0:
+                    cp(v("pb"), P)
+                ts(v("pi"), v("pb"), 255, A.bitwise_and)
+                ts(v("p2", 0, 128), X, 0.0, A.is_le)
                 tt(v("pd"), v("pi"), cs, A.subtract)
-                ts(v("p3", 0, 128), X, 0.0, A.is_le)
-                tt(v("pt"), v("p3", 0, 128), v("pd"), A.mult)
-                tt(ind(v("yp"), col), v("pt"), v("csf"), A.add)
                 if t > 0:
-                    cp(v("csf"), v("cs", 128 * t - 128, 128 * t))
                     level_open(t - 1, True)
+                tt(v("pt"), v("p2", 0, 128), v("pd"), A.mult)
+                if t > 0:
+                    redirect_b(t - 1)
                 if t == 2:
-                    ms(v("lev"), 3.0)
-                    for u in range(3):
-                        ms(v("lc", 128 * u, 128 * u + 128), float(u))
-                if t == 1:
-                    for u in range(3):
-                        cp(ind(v("lev"), v("co", 8 * u, 8 * u + 8)), v("lc", 128 * u, 128 * u + 128))
-                    for c in range(8):
-                        dma("Y", "ol", T.ylev[c:c + 1, :], T.lev[16 * c:16 * c + 1, :], [v("lev")], [])
+                    act(v("csf", 0, 256), v("cs", 0, 256), F.Copy)
+                tt(ind(v("yp"), col), v("pt"), v("csf", 128 * t, 128 * t + 128), A.add)
                 if t == 0:
                     dma("Y", "oy", T.yphi[:], T.yp[:], [v("yp")], [])
             else:
-                ts(v("kp"), X, 0.0, A.is_le)
-                if t == 0:
-                    tt(ind(own(s + 1), col), v("ams"), v("kp"), A.mult)
-                    send(s + 1)
-                else:
+                kp = v("kp", 128 * t, 128 * t + 128)
+                ts(kp, X, 0.0, A.is_le)
+                if t > 0:
                     level_open(t - 1, t > 1)
-                cp(v("als"), ind(v("al"), col))
-                tt(ind(v("al"), col), v("als"), v("kp"), A.mult)
-                if t == 1:
-                    tt(own(s + 2), own(0), v("al"), A.mult)
-                    cp(v("ams"), ind(own(s + 2), v("co", 0, 8)))
+                tt(ind(own(s0 + 6), col), v("asel", 128 * t, 128 * t + 128), kp, A.mult)
                 if t == 2 and ps == 0:
-                    for r in range(4):
-                        ms(v("pk", r, V, 4), (4 - r) / 16.0)
+                    lists_x(0, 1)
+                if t > 0:
+                    redirect_b(t - 1)
+                if t == 2 and ps == 0:
+                    const(v("al"), 1.0)
+                if t == 1:
+                    sel("alsel", v("al"), 0, 3)
                 if t == 0:
-                    ts(v("kb"), v("al"), -1.0, A.add)
-                    tt(v("rc"), v("kb"), v("pk"), A.mult)
+                    send(s + 1)
+                    tt(ind(v("al"), v("co")), v("alsel"), v("kp"), A.mult)
+                    for r in range(4):
+                        act(v("rc", r, V, 4), v("al", r, V, 4), F.Identity, (r - 4) / 16.0, (4 - r) / 16.0)
 
     count = {e: 0 for e in ENG}
     val = {}

import numpy as np
from concourse.bass import DstId, RemoteDMATransfer
from concourse.mybir import AluOpType as A, ActivationFunctionType as F

V, NR, NP = 512, 4, 3
W = V * NR
NS = 6 * NP
K = float(2 ** 42)
M1 = 1.5 * 2 ** 23
M8 = 1.5 * 2 ** 31
PAIRS = [(0, 1), (0, 2), (0, 3), (1, 2), (1, 3), (2, 3)]

bf, f32, i32, u16, f16 = "bfloat16", "float32", "int32", "uint16", "float16"
SB = {
    "tb": (NS * W, bf), "ampi": (V, i32), "phii": (V, i32), "trii": (V, i32), "thi": (1, i32), "tq": (V, i32),
    "tB": (V, i32), "tC": (V, f32), "tD": (V, f32), "li": (64, i32), "lu": (64, u16),
    "ab": (V, u16), "ab2": (256, u16), "phib": (V, bf), "gb": (4096, bf), "mn": (4096, bf),
    "di": (130, i32), "zero": (V, bf), "ti": (128, i32), "gg": (24, i32), "pc": (8, i32), "pf": (16, f32), "c64": (8, f32),
    "i1": (128, bf), "ie": (128, bf), "i2": (128, bf), "i3": (128, bf), "i4": (128, bf), "ni": (128, bf), "s8": (128, bf),
    "g1": (128, bf), "g2": (128, bf), "ng": (128, bf), "thm": (V, bf), "zz": (144, bf), "zq": (144, bf), "sm": (256, bf),
    "brow": (128, bf), "nlt": (V, bf), "nie": (128, bf), "rr": (256, bf), "lt": (V, bf), "lb": (V, bf), "eu": (V, bf),
    "ed": (V, bf), "lv": (384, bf),
    "pa0": (128, f16), "pa1": (128, f16), "pb0": (128, f16), "pb1": (128, f16), "i16": (128, f16),
    "cb": (256, bf), "cb2": (128, bf), "c25": (128, bf), "cd": (64, bf), "cm": (64, bf), "c128": (128, bf), "cap": (1, f32),
    "c49": (256, bf), "r256": (256, bf), "rs16": (256, bf), "thb": (2, bf), "thw": (4, i32), "b4": (16, f32),
    "cl": (128, bf), "t1": (V, i32), "t2": (V, bf), "x0": (V, bf), "x1": (V, bf), "yy": (V, bf), "rc": (V, bf), "al": (V, bf),
    "z": (128, f32), "zs": (128, f32), "zb": (256, bf), "zsb": (256, bf), "ff": (16, f32), "lhf": (16, f32), "lh": (16, u16),
    "cf": (8, f32), "co": (24, u16), "tsel": (256, f16), "ksel": (256, bf), "psel": (256, bf), "sk": (256, bf),
    "ll": (384, u16), "lf": (256, f32), "lq": (256, f16), "lz": (128, f32), "lr": (256, u16),
    "cs": (384, bf), "csf": (384, f32), "q": (1024, bf), "dw": (1024, bf), "aw": (1024, bf),
    "vc": (64, bf), "pi": (128, i32), "pq": (128, bf), "pb": (128, i32), "rk": (128, bf), "kp": (384, bf),
    "asel": (384, bf), "alsel": (384, bf), "pd": (128, bf), "pt": (128, f32), "yp": (V, f32), "lev": (V, f32),
}
SCRATCH = {n: ("sbuf", [128, w], d) for n, (w, d) in SB.items()}
for _b in range(8):
    SCRATCH["p%d" % _b] = ("psum", [128, 512], "float32")
DMAS = ["amp", "phi", "tri", "th", "la", "oy", "ol"]
SEMAPHORES = ["sV", "sS", "sP", "sG", "sent"] + ["d_" + d for d in DMAS] + ["arr%d" % s for s in range(NS)]


def rank_program(g, core, T, topo):
    rank = T.rank_of(core)
    if rank is None:
        return
    Q = {"V": g.vector, "S": g.scalar, "P": g.tensor, "G": g, "Y": g.sync}
    ENG = ["V", "S", "P", "G"]
    width = {n: w for n, (w, d) in SB.items()}
    width.update({"p%d" % b: 512 for b in range(8)})
    ops = []
    lastw = {n: np.full(w, -1) for n, w in width.items()}
    lastr = {n: {} for n in width}
    bank = {"p%d" % b: {} for b in range(8)}
    clock = {q: {} for q in Q}

    def v(n, a=0, b=None, s=1):
        return (n, a, width[n] if b is None else b, s)

    def ind(win, off):
        return ("*", win, off)

    def ap(x):
        if not isinstance(x, tuple):
            return x
        if x[0] == "*":
            return ap(x[1]).indirect(ap(x[2]))
        return T[x[0]][:, x[1]:x[2]] if x[3] == 1 else T[x[0]][:, x[1]:x[2]:x[3]]

    def rec(q, src, call, reads, writes, extra=()):
        me = len(ops)
        rd, wr = [], []
        for x in reads:
            if isinstance(x, tuple):
                rd += [x[1], x[2]] if x[0] == "*" else [x]
        for x in writes:
            if x[0] == "*":
                wr.append(x[1]); rd.append(x[2])
            else:
                wr.append(x)
        deps = set()
        for (n, a, b, s) in rd:
            deps.update(np.unique(lastw[n][a:b:s]).tolist())
        for (n, a, b, s) in wr:
            deps.update(np.unique(lastw[n][a:b:s]).tolist())
            for arr in lastr[n].values():
                deps.add(int(arr[a:b:s].max()))
        for (n, a, b, s) in rd + wr:
            if n in bank:
                deps.update(o for e, o in bank[n].items() if e != q)
        deps.discard(-1)
        best = {}
        for d in deps:
            sd = ops[d]["src"]
            if sd == "R" or (sd == "P" and src == "P"):
                continue
            best[sd] = max(best.get(sd, -1), d)
        waits = []
        ck = clock[q]
        for d in sorted(best.values(), reverse=True):
            sd = ops[d]["src"]
            if ck.get(sd, -1) >= d:
                continue
            waits.append(d)
            ops[d]["need"] = True
            ck[sd] = d
            for k2, v2 in ops[d]["clock"].items():
                ck[k2] = max(ck.get(k2, -1), v2)
        ops.append({"q": q, "src": src, "call": call, "waits": waits, "clock": dict(ck), "need": False, "extra": list(extra)})
        for (n, a, b, s) in rd:
            if src not in lastr[n]:
                lastr[n][src] = np.full(width[n], -1)
            lastr[n][src][a:b:s] = me
        for (n, a, b, s) in wr:
            lastw[n][a:b:s] = me
        for (n, a, b, s) in rd + wr:
            if n in bank:
                bank[n][q] = me
        return me

    pend = {"V": [], "S": []}

    def take(q):
        x = pend[q][:]
        del pend[q][:]
        return x

    def tt(o, a, b, op):
        rec("V", "V", lambda: g.vector.tensor_tensor(ap(o), ap(a), ap(b), op), [a, b], [o], take("V"))

    def ts(o, a, s1, op0, s2=None, op1=None):
        if op1 is None:
            rec("V", "V", lambda: g.vector.tensor_scalar(ap(o), ap(a), ap(s1), None, op0), [a, s1], [o], take("V"))
        else:
            rec("V", "V", lambda: g.vector.tensor_scalar(ap(o), ap(a), ap(s1), ap(s2), op0, op1), [a, s1, s2], [o], take("V"))

    def cp(o, a):
        rec("V", "V", lambda: g.vector.tensor_copy(ap(o), ap(a)), [a], [o], take("V"))

    def ms(o, c):
        rec("V", "V", lambda: g.vector.memset(ap(o), c), [], [o])

    def ms_hi(n, c):
        rec("V", "V", lambda: g.vector.memset(T[n][64:128, :], c), [], [v(n)])

    def scan(o, d0, d1, op0, op1):
        rec("V", "V", lambda: g.vector.tensor_tensor_scan(ap(o), ap(d0), ap(d1), 0.0, op0, op1), [d0, d1], [o])

    def act(o, a, func, bias=None, scale=1.0):
        if bias is None:
            rec("S", "S", lambda: g.scalar.activation(ap(o), ap(a), func), [a], [o], take("S"))
        else:
            rec("S", "S", lambda: g.scalar.activation(ap(o), ap(a), func, bias=ap(bias), scale=ap(scale)), [a, bias, scale], [o], take("S"))

    def const(o, c):
        act(o, v("zero", 0, (o[2] - o[1] + o[3] - 1) // o[3]), F.Identity, c)

    def times(o, a, c):
        act(o, a, F.Identity, 0.0, c)

    def mm(o, l, r, start=False, stop=False):
        l = v(l) if isinstance(l, str) else l
        rec("P", "P", lambda: g.tensor.matmul(ap(o), ap(l), ap(r), start, stop), [l, r], [o])

    def iota(o, pat, base, cm, fl=False):
        if fl:
            rec("G", "G", lambda: g.iota(ap(o), pat, base, cm, allow_small_or_imprecise_dtypes=True), [], [o])
        else:
            rec("G", "G", lambda: g.iota(ap(o), pat, base, cm), [], [o])

    def aff(o, a, pat, op, fill, base, cm):
        rec("G", "G", lambda: g.affine_select(ap(o), ap(a), pat, op, fill, base, cm), [a], [o])

    ndma = {d: 0 for d in DMAS}

    def dma(q, name, o, a, reads, writes):
        ndma[name] += 1
        rec(q, "d_" + name, lambda: Q[q].dma_start(o, a), reads, writes)

    peers = [c for c in T.cores if c != core]
    far = [c for c in peers if topo.chip(c) != topo.chip(core)]
    near = [c for c in peers if topo.chip(c) == topo.chip(core)]
    off_e = topo.engines(core, far[0])
    on_e = [e for e in topo.engines(core, near[0]) if e not in off_e]
    route = [(far, sum(1 << e for e in off_e)), (near, sum(1 << e for e in on_e))]
    per_send = len(off_e) + len(on_e)
    per_arr = len(far) * len(off_e) + len(near) * len(on_e)
    nsend = [0] * NS

    def own(s, a=0, b=V, st=1):
        return v("tb", s * W + rank * V + a, s * W + rank * V + b, st)

    def tab(s):
        return v("tb", s * W, (s + 1) * W)

    def new(s0, t):
        a = (s0 + 4) * W + (0 if t == 2 else V + 16) + 128 * rank
        return v("tb", a, a + 128)

    def send(s, a=0, b=V, x=None):
        x = x or own(s, a, b)
        nsend[s] += 1

        def call():
            tr = []
            for grp, m in route:
                ids = [DstId(rid=topo.addr(c)[0], pnc=topo.addr(c)[1]) for c in grp]
                tr.append(RemoteDMATransfer(dst_ids=ids, dma_engine_mask=m, remote_sem=T.sem["arr%d" % s],
                                            srcs=[ap(x)], dsts=[ap(x) for c in grp]))
            return g.remote_dma_fused(tr, local_sem=T.sem.sent)
        rec("G", "R", call, [x], [])

    def arrive(s):
        for q in pend:
            pend[q].append(("arr%d" % s, nsend[s] * per_arr))

    dma("Y", "amp", T.ampi[:, 0:256], T.amp[:, 0:256], [], [v("ampi", 0, 256)])
    dma("S", "amp", T.ampi[:, 256:512], T.amp[:, 256:512], [], [v("ampi", 256, 512)])
    for c in range(8):
        a, e = c // 2, c % 2
        dma("YS"[e], "la", T.tB[32 * a:32 * a + 32, 256 * e:256 * e + 256], T.tri[16 * c:16 * c + 16, :], [],
            [v("tB", 256 * e + a, 256 * e + 256, 4)])
    dma("Y", "th", T.thi[:], T.th[:], [], [v("thi")])
    dma("S", "phi", T.phii[:], T.phi[:], [], [v("phii")])
    dma("Y", "tri", T.trii[:], T.tri[:], [], [v("trii")])
    iota(v("pc", 0, 1), [[1, 1]], 0, 1)
    iota(v("di"), [[1, 130]], 128, -1)
    iota(v("gg"), [[0, 3], [16, 8]], 15, -1)
    iota(v("li", 0, 32), [[16, 16], [256, 2]], 0, 0)
    iota(v("li", 32, 64), [[2, 2], [1, 2], [4, 8]], 0, 0)
    iota(v("c64"), [[64, 8]], 0, 0, True)
    d128 = v("di", 0, 128)
    ms(v("zero"), 0.0)
    ms(v("lt"), 0.0)
    ms(v("cd"), -31.0 / 64)
    ms(v("cm"), M1)
    ms(v("cap"), 255.0)
    ts(v("pc", 1, 2), v("pc", 0, 1), 15, A.bitwise_and)
    ms_hi("cd", -1.0)
    ms_hi("cm", 0.0)
    ms_hi("cap", 1.0)
    ts(v("i1"), d128, 128.0, A.is_equal)
    ts(v("ti"), d128, 15, A.bitwise_and)
    ts(v("gg"), v("gg"), 4, A.arith_shift_right)
    cp(v("pf", 0, 1), v("pc", 1, 2))
    ts(v("pf", 1, 2), v("pc", 1, 2), 32.0, A.mult)
    ts(v("pf", 2, 3), v("pc", 0, 1), 64.0, A.is_lt, 32.0, A.mult)
    ts(v("pf", 3, 4), v("pc", 0, 1), 64.0, A.is_ge, 128.0, A.mult)
    ts(v("lu", 0, 32), v("li", 0, 32), v("pf", 0, 1), A.add)
    cp(own(0), v("ampi"))
    send(0)
    const(v("cb"), -31.0 / 64)
    for r in range(4):
        const(v("r256", r, 256, 4), 256.0 * r)
    times(v("ie"), v("i1"), 0.125)
    times(v("ni"), v("i1"), -1.0)
    const(v("lb"), 0.0)
    const(v("rs16"), 1.0)
    const(v("rs16", 0, 256, 16), 0.0)
    iota(v("brow"), [[1, 128]], 0, 0, True)
    iota(v("g2"), [[0, 128]], 1, 0, True)
    aff(v("ng"), v("g2"), [[-16, 8], [0, 16]], A.is_ge, 0.0, 0, 1)
    aff(v("g1"), v("ng"), [[16, 8], [0, 16]], A.is_ge, 0.0, 15, -1)
    ts(v("lu", 32, 64), v("li", 32, 64), v("pf", 1, 2), A.add)
    for r in range(4):
        ts(v("lt", 144 * r, 144 * r + 16), v("ti", 0, 16), 0.0, A.is_equal, 1.0 / 32, A.mult)
        qs = [(q, 2.0 if a == r else -2.0) for q, (a, b) in enumerate(PAIRS) if r in (a, b)]
        runs = []
        for q, sg in qs:
            if runs and runs[-1][1] == q and runs[-1][2] == sg:
                runs[-1][1] = q + 1
            else:
                runs.append([q, q + 1, sg])
        for q0, q1, sg in runs:
            ts(v("lt", 128 * r + 64 + 8 * q0, 128 * r + 64 + 8 * q1), v("gg", 0, 8 * (q1 - q0)), 0.0, A.is_equal, sg, A.mult)
    for r in range(4):
        mm(v("p7", 128 * r, 128 * r + 128), v("lt", 128 * r, 128 * r + 128), v("i1"), True, True)
    times(v("eu"), v("p7"), v("pf", 2, 3))
    times(v("ed"), v("p7"), v("pf", 3, 4))
    cp(v("tC"), ind(v("tB"), v("lu", 0, 32)))
    rec("V", "V", lambda: g.vector.transpose(T.tD[:], T.tC[:]), [v("tC")], [v("tD")])
    cp(v("ab"), ind(v("tD"), v("lu", 32, 64)))
    ts(v("sm", 0, 128), v("ti"), 0.0, A.is_equal)
    ts(v("pc", 2, 3), v("pc", 0, 1), 1, A.bitwise_and)
    ts(v("pf", 4, 5), v("pc", 1, 2), 4.0, A.mult)
    ts(v("pf", 15, 16), v("pc", 1, 2), 4.0, A.mult, 3.0, A.add)
    ts(v("pf", 14, 15), v("pc", 1, 2), 0.0, A.is_equal)
    cp(v("pf", 7, 8), v("thi"))
    cp(v("pf", 5, 6), v("pc", 2, 3))
    ts(v("pf", 6, 7), v("pc", 2, 3), 0.0, A.is_equal)
    ts(v("tq"), v("trii"), 2, A.arith_shift_right)
    cp(v("phib"), v("phii"))
    times(v("nlt"), v("lt"), -1.0)
    times(v("nie"), v("i1"), -0.125)
    for r in range(4):
        times(v("lb", 128 * r + 64, 128 * r + 112), v("lt", 128 * r + 64, 128 * r + 112), 65536.0)
    for r in (2, 3, 4):
        times(v("i%d" % r), v("i1"), float(r))

    def consts0():
        const(v("thb"), v("pf", 7, 8))
        mm(v("p5", 256, 258), "g1", v("thb"), True, True)
        act(v("b4", 0, 8), v("c64"), F.Identity, v("pf", 4, 5))
        act(v("b4", 8, 16), v("c64"), F.Identity, v("pf", 15, 16))
        const(v("c25"), -2.5)
        times(v("ng"), v("g1"), -1.0)
        times(v("pq"), v("sm", 0, 128), 1.0 / 64)
        const(v("zq"), v("pf", 14, 15))

    def consts1():
        aff(v("s8"), v("pq"), [[1, 128]], A.not_equal, 9.0 / 64, 0, -1)
        aff(v("zz"), v("zq"), [[1, 144]], A.is_equal, 0.0, -16, -1)
        cp(v("thw", 0, 2), v("p5", 256, 258))
        ts(v("pa0"), d128, 128.0, A.is_equal, v("pf", 6, 7), A.mult)
        ts(v("pa1"), d128, 129.0, A.is_equal, v("pf", 6, 7), A.mult)
        ts(v("thw", 2, 3), v("thw", 0, 1), 4, A.arith_shift_right)
        ts(v("thw", 3, 4), v("thw", 0, 1), 15, A.bitwise_and)
        ts(v("pb0"), d128, 127.0, A.is_equal, v("pf", 5, 6), A.mult)
        ts(v("pb1"), d128, 128.0, A.is_equal, v("pf", 5, 6), A.mult)
        ts(v("pf", 8, 9), v("pc", 1, 2), 8.0, A.is_lt)
        ts(v("pf", 9, 10), v("pc", 1, 2), 8.0, A.is_ge)
        for h in range(2):
            ts(v("pf", 10 + 2 * h, 11 + 2 * h), v("thw", 2, 3), -16.0, A.mult, v("pf", 8 + h, 9 + h), A.mult)
            ts(v("pf", 11 + 2 * h, 12 + 2 * h), v("thw", 3, 4), -1.0, A.mult, v("pf", 8 + h, 9 + h), A.mult)
        times(v("sm", 128, 256), v("sm", 0, 128), 1.0)
        const(v("c49"), 49152.0)
        const(v("cb2"), -63.0 / 128)
        times(v("zq"), v("zz"), 528.0 / K)

    def consts2():
        for u in range(4):
            times(v("thm", 128 * u, 128 * u + 128), v("g1"), v("pf", 10 + u, 11 + u))
        times(v("g2"), v("g1"), 2.0)
        const(v("c128"), -128.0)

    def sel(n, src, t, k=1):
        act(v(n, 128 * t, 128 * (t + k)), ind(src, v("co", 8 * t, 8 * (t + k))), F.Copy)

    def lists(t):
        cp(v("ll", 128 * t, 128 * t + 128), ind(v("trii"), v("co", 8 * t, 8 * t + 8)))

    def lists_x(t, part=None):
        col = v("co", 8 * t, 8 * t + 8)
        if part != 1:
            cp(v("lf", 128 * t, 128 * t + 128), ind(v("trii"), col))
        if part != 0:
            ts(v("lq", 128 * t, 128 * t + 128), ind(v("tq"), col), -1664.0, A.add)

    def redirect_a(s0, t):
        G = lambda a, b: (v("gb", 16 * a, 16 * b), ind(tab(s0 + 3), v("ll", 128 * t + a, 128 * t + b)))
        act(*G(0, 64), F.Copy)
        cp(*G(64, 96))
        act(*G(96, 128), F.Copy)

    def redirect_p(t, h):
        if h == 0:
            mm(v("p3", 384, 512), "i16", v("lq", 128 * t, 128 * t + 128), True)
            mm(v("p3", 384, 512), "i4", v("c128"))
        for x in range(16):
            mm(v("p3", 384 + 64 * h, 448 + 64 * h), v("zq", 16 - x, 144 - x), v("gb", 1024 * h + x, 1024 * h + 1024, 16), False, h == 1 and x == 15)

    def redirect_b(t):
        tt(v("lz"), v("p3", 384, 512), v("lf", 128 * t, 128 * t + 128), A.max)
        ts(v("lr", 128 * t, 128 * t + 128), v("lz"), float(W + V if t else 4 * W), A.min)

    def level_prep(t, js=range(4)):
        for j in js:
            mm(v("p%d" % (4 + j), 0, 256), "i1", v("c49"), True)
            for m in range(4):
                mm(v("p%d" % (4 + j), 64 * m, 64 * m + 64), "ni", v("cs", 128 * t + 64 * (j // 2), 128 * t + 64 * (j // 2) + 64))

    def level_open(t, phase):
        mm(v("p1", 0, 128), "i1", v("cb2"), True)
        if phase:
            mm(v("p0", 0, 128), "i1", v("cb2"), True)
            mm(v("p0", 0, 128), "i1", v("cs", 128 * t, 128 * t + 128))

    def gat(s, lst, second, c0, c1):
        h = c0
        if c0 == 0:
            h = c1 // 2
            cp(v("gb", 0, 16 * h), ind(tab(s), v(lst, second, second + h)))
        act(v("gb", 16 * h, 16 * c1), ind(tab(s), v(lst, second + h, second + c1)), F.Copy)
        tt(v("mn", 16 * c0, 16 * c1), ind(tab(s), v(lst, c0, c1)), v("gb", 16 * c0, 16 * c1), A.min)

    PS = lambda h: v("p%d" % h, 0, 256)
    DU = lambda h: v("p%d" % (2 + h), 0, 64)
    PU = lambda h, r=0, st=1: v("p%d" % (4 + h), r, 256, st)
    PD = lambda h, r=0, st=1: v("p%d" % (6 + h), r, 256, st)
    wt = lambda n, r: v(n, 128 * r, 128 * r + 128)

    def full_round(s, biases, slack):
        for h in range(2):
            mm(PS(h), "i1", v("cb"), True)
            mm(DU(h), "i1", v("cd"), True)
            for kb in biases:
                for r in range(4):
                    mm(DU(h), wt("lb", r), v(kb, 256 * h + r, 256 * h + 256, 4))
        for h in range(2):
            mm(PD(h), "i1", v("r256"), True)

        def add(h, x, a, l4, l1, end=False):
            for r in range(4):
                mm(DU(h), wt(l4, r), v(x, a + r, a + 256, 4))
            if end:
                mm(DU(h), "i1", v("cm"))
                mm(DU(h), "ni", v("cm"), False, True)
            mm(PS(h), l1, v(x, a, a + 256), False, end)

        def piece(h, m0, m1):
            gat(s, "ab", 256, 128 * h + 16 * m0, 128 * h + 16 * m1)
            for m in range(m0, m1):
                add(h, "mn", 2048 * h + 256 * m, "lt", "ie", m == 7)

        def clamp(h):
            c = v("cl", 64 * h, 64 * h + 64)
            ts(c, DU(h), 0.0, A.max, v("cap"), A.min)
            for r in range(4):
                mm(PU(h, r, 4), wt("eu", r), c, True, True)
            for r in range(4):
                mm(PD(h, r, 4), wt("ed", r), c, False, r == 3)

        hf = lambda n, h: v(n, 256 * h, 256 * h + 256)
        m1 = lambda h: tt(hf("t1", h), PS(h), own(s, 256 * h, 256 * h + 256), A.min)
        m2 = lambda h: tt(hf("t2", h), PU(h), hf("t1", h), A.min)
        m3 = lambda h: tt(own(s + 1, 256 * h, 256 * h + 256), PD(h), hf("t2", h), A.min)

        arrive(s)
        for m in range(0, 8, 2):
            piece(0, m, m + 2)
        piece(1, 0, 2)
        clamp(0)
        m1(0)
        piece(1, 2, 4)
        m2(0)
        gat(s, "ab", 256, 192, 224)
        x, y = v("mn", 3840, 4096), v("gb", 3840, 4096)
        act(y, ind(tab(s), v("ab", 496, 512)), F.Copy)
        act(x, ind(tab(s), v("ab", 240, 256)), F.Copy)
        m3(0)
        send(s + 1, 0, 256)
        gat(s, "ab", 256, 224, 240)
        mm(v("p5", 256, 512), "i1", x, True)
        mm(v("p5", 256, 512), "ni", y, False, True)
        act(v("rr"), v("p5", 256, 512), F.Relu)
        for m in (7, 4, 5):
            add(1, "mn", 2048 + 256 * m, "lt", "ie")
        add(1, "rr", 0, "nlt", "nie")
        add(1, "mn", 2048 + 256 * 6, "lt", "ie", True)
        slack()
        clamp(1)
        m1(1)
        m2(1)
        m3(1)
        send(s + 1, 256, 512)

    def mark(x, h):
        act(v(x, 256 * h, 256 * h + 256), PD(h), F.Relu, 1.0, -1.0 / 256)

    def gone(x):
        o = v("p3", 256, 384)
        mm(o, "i4", v("brow"), True)
        for r in (1, 2, 3):
            mm(o, "i%d" % r, v(x, r, V, 4), False, r == 3)

    def gone_list(t):
        return [lambda: tt(v("z"), v("p3", 256, 384), v("sm", 0, 128), A.mult),
                lambda: scan(v("zs"), v("rs16", 0, 128), v("z"), A.mult, A.add),
                lambda: cp(v("co", 8 * t, 8 * t + 8), v("zs", 15, 128, 16))]

    for ps in range(NP):
        s0 = 6 * ps
        last = ps == NP - 1

        def slack0():
            mark("x0", 0)
            if ps == 0:
                consts0()
            if not last:
                act(own(s0 + 6), own(s0), F.Copy)
            else:
                act(v("yp"), v("phib"), F.Copy)
                for u, c in enumerate((-1.0 / (8 * K), -23.0 / 8, -7.0 / 8)):
                    times(wt("lv", u), v("i1"), c)

        def fill(h):
            act(own(s0 + 3, 256 * h, 256 * h + 256), PD(h), F.Abs, 9 * K, -10 * K / 768)

        def slack1():
            act(v("yy", 0, 256), PD(0), F.Abs, -1.5, 1.0 / 256)
            fill(0)
            mark("x1", 0)
            sel("cs", v("phib"), 0)
            if not last:
                sel("asel", own(s0), 0)

        full_round(s0, ["rc"] if ps else [], slack0)
        mark("x0", 1)
        gone("x0")
        ms(v("tb", (s0 + 4) * W + V, (s0 + 4) * W + V + 16), K)
        if ps == 0:
            consts1()
        for f in gone_list(0):
            f()
        lists(0)
        if ps:
            lists_x(0)
        full_round(s0 + 1, ["x0", "rc"] if ps else ["x0"], slack1)

        def left_a(h):
            if h:
                act(v("yy", 256, 512), PD(1), F.Abs, -1.5, 1.0 / 256)
            b = "p%d" % (2 + h)
            mm(v(b, 0, 128), "i1", v("c25"), True)
            for e, (r2, r1) in enumerate(((0, 1), (3, 2))):
                mm(v(b, 64 * e, 64 * e + 64), "i2", v("yy", 256 * h + r2, 256 * h + 256, 4))
                mm(v(b, 64 * e, 64 * e + 64), "i1", v("yy", 256 * h + r1, 256 * h + 256, 4), False, e == 1)

        def left_b(h):
            a = 128 * h
            return [
                lambda: tt(v("zb", a, a + 128), v("p%d" % (2 + h), 0, 128), v("sm", 0, 128), A.mult),
                lambda: scan(v("zsb", a, a + 128), v("rs16", 0, 128), v("zb", a, a + 128), A.mult, A.max),
                lambda: (tt(v("lhf", 8 * h, 8 * h + 4), v("zsb", a + 15, a + 64, 16), v("b4", 4 * h, 4 * h + 4), A.add),
                         tt(v("lhf", 8 * h + 4, 8 * h + 8), v("b4", 8 + 4 * h, 12 + 4 * h), v("zsb", a + 79, a + 128, 16), A.subtract)),
                lambda: cp(v("lh", 8 * h, 8 * h + 8), v("lhf", 8 * h, 8 * h + 8)),
                lambda: cp(v("tsel", a, a + 128), ind(v("trii"), v("lh", 8 * h, 8 * h + 8))),
            ]

        def left_c(h):
            a = 128 * h
            b = "p%d" % (4 * h)
            for j, (l0, l1) in enumerate((("pa0", "pa1"), ("pb0", "pb1"))):
                o = v(b, 64 * j, 64 * j + 64)
                mm(o, l0, v("tsel", a, a + 64), True)
                mm(o, l1, v("tsel", a + 64, a + 128), False, True)

        def left_d(h):
            cp(v("ab2", 128 * h, 128 * h + 128), v("p%d" % (4 * h), 0, 128))

        def left_s(h):
            a, l = 128 * h, v("lh", 8 * h, 8 * h + 8)
            if ps:
                times(v("ksel", a, a + 128), ind(v("rc"), l), float(2 ** 21))
            act(v("psel", a, a + 128), ind(v("phib"), l), F.Copy)

        left_a(0)
        left_a(1)
        la, lb_ = left_b(0), left_b(1)
        for f in (la[0], la[1], la[2], lb_[0], la[3], lb_[1], la[4], lb_[2]):
            f()
        left_s(0)
        left_c(0)
        lb_[3]()
        left_d(0)
        lb_[4]()
        left_s(1)
        left_c(1)
        s = s0 + 2
        arrive(s)

        def bias2(h):
            if ps:
                mm(v("p%d" % h, 0, 64), "i1", v("ksel", 128 * h, 128 * h + 64), True)
                mm(v("p%d" % h, 0, 64), "ni", v("ksel", 128 * h + 64, 128 * h + 128))

        def gat2(h, c0, c1):
            a, b, o = 128 * h + c0, 128 * h + c1, 1024 * h
            k = c0
            if h == 0 and c0 == 0:
                k = c1 // 2
                cp(v("gb", 0, 16 * k), ind(tab(s), v("ab2", 64, 64 + k)))
                left_d(1)
            act(v("gb", o + 16 * k, o + 16 * c1), ind(tab(s), v("ab2", 128 * h + 64 + k, b + 64)), F.Copy)
            tt(v("mn", o + 16 * c0, o + 16 * c1), ind(tab(s), v("ab2", a, b)), v("gb", o + 16 * c0, o + 16 * c1), A.min)

        def pe2(h):
            for j in range(16):
                mm(v("p%d" % h, 0, 64), "ng" if j % 2 else "g1", v("mn", 1024 * h + j, 1024 * h + 1024, 16), j == 0 and ps == 0, j == 15)

        def post2(h):
            a = 128 * h
            for e, op in ((0, A.is_le), (1, A.is_gt)):
                ts(v("sk", a + 64 * e, a + 64 * e + 64), v("p%d" % h, 0, 64), 0.0, op, 8 * K, A.mult)
            tt(ind(own(s + 1), v("lh", 8 * h, 8 * h + 8)), v("psel", a, a + 128), v("sk", a, a + 128), A.add)

        bias2(0)
        bias2(1)
        gat2(0, 0, 32)
        gat2(0, 32, 64)
        pe2(0)
        gat2(1, 0, 32)
        gat2(1, 32, 64)
        fill(1)
        mark("x1", 1)
        if ps == 0:
            consts2()
        pe2(1)
        post2(0)
        post2(1)
        send(s + 1)
        gone("x1")
        if last:
            for u, x in enumerate((own(s0 + 3), v("x0"), v("x1"))):
                mm(v("p2"), wt("lv", u), x, u == 0, u == 2)
        gl = gone_list(1)
        tt(v("zb"), v("sk"), v("sm"), A.mult)
        gl[0]()
        scan(v("zsb"), v("rs16"), v("zb"), A.mult, A.add)
        gl[1]()
        tt(v("ff"), v("zsb", 15, 256, 16), v("lhf"), A.mult)
        gl[2]()
        for h in range(2):
            tt(v("cf", 4 * h, 4 * h + 4), v("ff", 8 * h, 8 * h + 4), v("ff", 8 * h + 4, 8 * h + 8), A.add)
        lists(1)
        ts(v("co", 16, 24), v("cf"), 1.0 / (8 * K), A.mult)
        sel("cs", v("phib"), 1)
        if ps == 0:
            ts(v("i16"), d128, 128.0, A.is_equal)
        lists_x(1)
        sel("cs", v("phib"), 2)
        lists(2)
        level_prep(2)
        level_open(2, True)
        if not last:
            sel("asel", own(s0), 1, 2)
        else:
            act(v("csf", 256, 384), v("cs", 256, 384), F.Copy)
            act(v("lev"), v("p2"), F.Identity, 3.0)
            for c in range(8):
                dma("Y", "ol", T.ylev[c:c + 1, :], T.lev[16 * c:16 * c + 1, :], [v("lev")], [])
        if ps == 0:
            lists_x(0, 0)
        for t in (2, 1, 0):
            s = s0 + 5 - t
            col = v("co", 8 * t, 8 * t + 8)
            cs = v("cs", 128 * t, 128 * t + 128)
            phase = last or t > 0
            arrive(s)
            E = lambda j: v("p%d" % (4 + j), 0, 256)
            H = lambda n, j, k=1: v(n, 256 * j, 256 * (j + k))
            win = v("tb", (s0 + 3) * W, (s0 + 4) * W + (0, V + 16, 2 * V + 16)[2 - t])
            G = lambda a, b: (v("gb", 16 * a, 16 * b), ind(win, v("lr" if t < 2 else "ll", 128 * t + a, 128 * t + b)))
            for h in range(2):
                cp(*G(64 * h, 64 * h + 32))
                act(*G(64 * h + 32, 64 * h + 64), F.Copy)
                for m in range(8):
                    for u in range(2):
                        mm(v("p%d" % (4 + 2 * h + m // 4), 64 * (m % 4), 64 * (m % 4) + 64), "i1",
                           v("gb", 1024 * h + 2 * m + u, 1024 * h + 1024, 16), False, m % 4 == 3 and u == 1)

            def sums(b, j, l, src, stop=False):
                if b == "p1" or phase:
                    for m in range(4):
                        mm(v(b, 64 * (j // 2), 64 * (j // 2) + 64), l, v(src, 256 * j + 64 * m, 256 * j + 64 * m + 64), False, stop and m == 3)

            def flags(j):
                for x in range(4 * j, 4 * j + 4):
                    mm(v("p2", 0, 64), v("zz", 16 - x, 144 - x), v("q", 64 * x, 64 * x + 64), x == 0, x == 15)

            dw = lambda j: tt(H("dw", j), E(j), H("q", j), A.subtract)
            for j in (1, 2, 3):
                act(H("q", j), E(j), F.Identity, 0.5)
            ts(H("q", 0), E(0), 0.5, A.add)
            flags(0)
            for j in range(2):
                dw(j)
                act(H("aw", j), H("dw", j), F.Abs)
                sums("p0", j, "s8", "dw")
                flags(j + 1)
            flags(3)
            dw(2)
            sums("p0", 2, "s8", "dw")
            sums("p1", 2, "ng", "dw")
            sums("p1", 0, "g1", "aw")
            dw(3)
            sums("p0", 3, "s8", "dw", True)
            sums("p1", 3, "ng", "dw")
            ts(v("vc"), v("p2", 0, 64), float(2 ** 20), A.is_lt)
            for h in range(2):
                for u in range(2):
                    mm(v("p1", 64 * h, 64 * h + 64), wt("thm", 2 * h + u), v("vc"))
            sums("p1", 1, "g1", "aw")
            ts(H("aw", 2, 2), H("dw", 2, 2), 0.0, A.max)
            sums("p1", 2, "g2", "aw")
            sums("p1", 3, "g2", "aw", True)
            X, P = v("p1", 0, 128), v("p0", 0, 128)
            if t > 0:
                ts(v("pq"), P, M8, A.add, M8, A.subtract)
                tt(v("pb"), P, v("pq"), A.subtract)
                ts(v("rk"), X, 0.0, A.is_gt, K, A.mult)
                tt(new(s0, t), v("pb"), v("rk"), A.add)
                send(s + 1, x=new(s0, t))
                redirect_a(s0, t - 1)
                redirect_p(t - 1, 0)
                level_prep(t - 1, (0,))
                redirect_p(t - 1, 1)
                level_prep(t - 1, (1, 2, 3))
            if last:
                if t == 0:
                    cp(v("pb"), P)
                ts(v("pi"), v("pb"), 255, A.bitwise_and)
                ts(v("p2", 0, 128), X, 0.0, A.is_le)
                tt(v("pd"), v("pi"), cs, A.subtract)
                if t > 0:
                    level_open(t - 1, True)
                tt(v("pt"), v("p2", 0, 128), v("pd"), A.mult)
                if t > 0:
                    redirect_b(t - 1)
                if t == 2:
                    act(v("csf", 0, 256), v("cs", 0, 256), F.Copy)
                tt(ind(v("yp"), col), v("pt"), v("csf", 128 * t, 128 * t + 128), A.add)
                if t == 0:
                    dma("Y", "oy", T.yphi[:], T.yp[:], [v("yp")], [])
            else:
                kp = v("kp", 128 * t, 128 * t + 128)
                ts(kp, X, 0.0, A.is_le)
                if t > 0:
                    level_open(t - 1, t > 1)
                tt(ind(own(s0 + 6), col), v("asel", 128 * t, 128 * t + 128), kp, A.mult)
                if t == 2 and ps == 0:
                    lists_x(0, 1)
                if t > 0:
                    redirect_b(t - 1)
                if t == 2 and ps == 0:
                    const(v("al"), 1.0)
                if t == 1:
                    sel("alsel", v("al"), 0, 3)
                if t == 0:
                    send(s + 1)
                    tt(ind(v("al"), v("co")), v("alsel"), v("kp"), A.mult)
                    for r in range(4):
                        act(v("rc", r, V, 4), v("al", r, V, 4), F.Identity, (r - 4) / 16.0, (4 - r) / 16.0)

    count = {e: 0 for e in ENG}
    val = {}
    for i, o in enumerate(ops):
        q, src = Q[o["q"]], o["src"]
        for d in o["waits"]:
            q.wait_ge(*val[d])
        for name, n in o["extra"]:
            q.wait_ge(T.sem[name], n)
        ins = o["call"]()
        if src.startswith("d_"):
            ins.then_inc(T.sem[src], 16)
            val[i] = (T.sem[src], 16 * ndma[src[2:]])
        elif src != "R" and o["need"]:
            count[src] += 1
            ins.then_inc(T.sem["s" + src], 1)
            val[i] = (T.sem["s" + src], count[src])
    g.wait_ge(T.sem.sent, sum(nsend) * per_send)
    g.sync.wait_ge(T.sem.d_ol, 16 * ndma["ol"])
    g.sync.wait_ge(T.sem.d_oy, 16 * ndma["oy"])
